import numpy as np
import ml_dtypes


def mxq(x, axis, fmt="e4m3"):
    dtype, down = {"e4m3": (ml_dtypes.float8_e4m3fn, 7), "e5m2": (ml_dtypes.float8_e5m2, 14)}[fmt]
    v = np.moveaxis(np.asarray(x, np.float32).astype(ml_dtypes.bfloat16).astype(np.float64), axis, -1)
    blocks = v.reshape(v.shape[:-1] + (-1, 32))
    amax = np.abs(blocks).max(-1, keepdims=True)
    byte = np.maximum(np.where(amax > 0, np.frexp(amax)[1] - 1 + 127, 0) - down, 1)
    scale = np.exp2(byte - 127.0)
    codes = (blocks / scale).astype(np.float32).astype(dtype).astype(np.float64)
    return np.moveaxis((codes * scale).reshape(v.shape), -1, axis)


WIDE = False


def mx_kscale(k):
    if not WIDE:
        return np.ones(k)
    levels = np.array([10, -10, 5, -5, 0])
    if k % 512:
        return np.exp2(np.random.permutation(np.resize(levels, k // 32))).repeat(32)
    a = np.empty((k // 512, 16))
    for p in range(k // 512):
        a[p, :8] = np.random.permutation(np.resize(levels, 8))
        for g in range(8):
            far = levels[np.abs(levels - a[p, g]) >= 10]
            a[p, g + 8] = far[np.random.randint(len(far))]
    return np.exp2(a.ravel()).repeat(32)


def f64(x):
    return np.asarray(x).astype(np.float64)


def striped(idx):
    return np.tile(np.asarray(idx).reshape(-1, 16).T, (8, 1)).astype(np.uint16)


def unstriped(offs):
    return offs[:16].T.reshape(-1).astype(np.int64)


E2M1 = np.array([0.0, 0.5, 1.0, 1.5, 2.0, 3.0, 4.0, 6.0, -0.0, -0.5, -1.0, -1.5, -2.0, -3.0, -4.0, -6.0])


def pack_weight(w, fmt):
    k, n = w.shape
    w = f64(np.asarray(w, np.float32).astype(ml_dtypes.bfloat16)).reshape(k // 32, 32, n)
    amax = np.abs(w).max(1)
    if fmt == "e4m3":
        byte = np.frexp(amax)[1] - 1 + 127 - 7
    else:
        mant, ex = np.frexp(amax / 6.0)
        byte = np.where(mant > 0.5, ex, ex - 1) + 127
    byte = np.clip(np.where(amax > 0, byte, 1), 1, 254)
    scaled = (w * np.exp2(127.0 - byte)[:, None, :]).reshape(k, n).astype(np.float32)
    by_word = np.ascontiguousarray(scaled.reshape(k // 512, 128, 4, n).transpose(0, 1, 3, 2))
    if fmt == "e4m3":
        words = by_word.astype(ml_dtypes.float8_e4m3fn).view(np.uint8)
    else:
        c = by_word.astype(ml_dtypes.float4_e2m1fn).view(np.uint8) & 0xF
        words = (c[..., 0::2] | (c[..., 1::2] << 4)).reshape(k // 512, 128, 2 * n)
    return np.ascontiguousarray(words), np.ascontiguousarray(byte.astype(np.uint8).reshape(k // 512, 16, n))


def unpack_weight(words, scales, fmt):
    g, _, n = scales.shape
    words = np.ascontiguousarray(words).reshape(g, 128, n, -1)
    if fmt == "e4m3":
        vals = words.view(ml_dtypes.float8_e4m3fn).astype(np.float64)
    else:
        nib = np.empty((g, 128, n, 4), np.uint8)
        nib[..., 0::2] = words & 0xF
        nib[..., 1::2] = words >> 4
        vals = E2M1[nib]
    vals = vals * np.repeat(np.exp2(scales.astype(np.float64) - 127.0), 8, axis=1)[..., None]
    return vals.transpose(0, 1, 3, 2).reshape(g * 512, n)


B, N, T, D, NQ = 1, 1024, 4096, 1024, 128
SEG = 16


def setup_inputs():
    n = np.random.standard_normal
    pages = np.random.permutation(T // 16)[:B * N // 16]
    idx = (pages[:, None] * 16 + np.arange(16)[None, :]).reshape(-1)
    s = mx_kscale(D)[:, None]
    kp = pack_weight(n((D, T)) / s, "e2m1")
    return {
        "qT": (n((B, D, NQ)) * s * (1.00 / np.sqrt(D))).astype(np.float32),
        "k_words": np.ascontiguousarray(kp[0].reshape(1, 2, 128, T, 2).transpose(0, 2, 3, 1, 4)).reshape(1, 128, T, 4),
        "k_scales": kp[1],
        "kn": np.tile(np.random.uniform(4.0, 8.0, 4096), (128, 1)).astype(np.float32),
        "qn": (np.random.uniform(4.0, 8.0, (B, NQ, 1))).astype(np.float32),
        "offs": striped(idx),
    }


def reference(qT, k_words, k_scales, kn, qn, offs):
    idx = unstriped(offs)
    pick = lambda x, which: x[:, which].reshape(x.shape[0], B, -1).transpose(1, 0, 2)
    k = unpack_weight(k_words.reshape(1, 128, T, 2, 2).transpose(0, 3, 1, 2, 4).reshape(2, 128, 2 * T), k_scales, "e2m1")
    kg = pick(k, idx)
    qq = mxq(f64(qT), 1, "e4m3")
    a = qq.transpose(0, 2, 1) @ kg
    y = f64(qn) - (2.0 * a - pick(f64(kn), idx)[:, :1, :]).reshape(B, NQ, N // SEG, SEG).max(-1)
    return y

@@ -1,0 +1,144 @@
+from contextlib import ExitStack
+
+import concourse.mybir as mybir
+from concourse.masks import make_identity
+
+F32 = mybir.dt.float32
+BF16 = mybir.dt.bfloat16
+I32 = mybir.dt.int32
+U32 = mybir.dt.uint32
+U16 = mybir.dt.uint16
+U8 = mybir.dt.uint8
+FP8X4 = mybir.dt.float8_e4m3fn_x4
+FP4X4 = mybir.dt.float4_e2m1fn_x4
+ALU = mybir.AluOpType
+ACT = mybir.ActivationFunctionType
+AXIS = mybir.AxisListType
+
+P = 128
+N, T, D, NQ, SEG = 1024, 4096, 1024, 128, 16
+PASSES = D // 512
+HALF = 512
+HALVES = N // HALF
+BLOCKS = HALF // P
+KN_ROW = P - 1
+SC0, SC_STEP = 32, 4
+
+FLOPS = 2 * NQ * N * D
+BYTES = 4 * D * NQ + 4 * P * T + 2 * 16 * T + 4 * T + 4 * NQ + 2 * P * (N // 16) + 4 * NQ * (N // SEG)
+
+
+def tile_attend_celldist_kernel(tc, qT, k_words, k_scales, kn, qn, offs, out):
+    nc = tc.nc
+    with ExitStack() as ctx:
+        sb = ctx.enter_context(tc.tile_pool(name="sb", bufs=1))
+        ps = ctx.enter_context(tc.psum_pool(name="ps", bufs=1))
+
+        offsets = sb.tile([P, N // 16], U16, name="offsets")
+        nc.sync.dma_start(offsets[:], offs)
+
+        scale_win = sb.tile([P, PASSES, T // 4], I32, name="scale_win")
+        nc.vector.memset(scale_win[:], 0)
+        nc.scalar.dma_start(
+            scale_win[SC0 : SC0 + 16 * SC_STEP : SC_STEP, :, :],
+            k_scales.rearrange("o f t -> f o t").bitcast(I32),
+        )
+        kn_win = sb.tile([P, T], F32, name="kn_win")
+        nc.scalar.dma_start(kn_win[KN_ROW:P, :], kn[0:1, :])
+        qn_col = sb.tile([P, 1], F32, name="qn_col")
+        nc.scalar.dma_start(qn_col[:], qn[0])
+
+        word_win = sb.tile([P, T], I32, name="word_win")
+        nc.sync.dma_start(word_win[:], k_words[0].rearrange("p t b -> p (t b)").bitcast(I32))
+        q_raw = []
+        for o in range(PASSES):
+            raw = sb.tile([P, 4, NQ], F32, name=f"q_raw{o}")
+            nc.sync.dma_start(raw[:], qT[0, 512 * o : 512 * (o + 1), :].rearrange("(p j) w -> p j w", j=4))
+            q_raw.append(raw)
+
+        ident = sb.tile([P, P], F32, name="ident")
+        make_identity(nc, ident[:])
+        nc.vector.memset(kn_win[0:KN_ROW, :], 0.0)
+
+        def half_offsets(h):
+            return offsets[:, h * (HALF // 16) : (h + 1) * (HALF // 16)]
+
+        kq = []
+        for h in range(HALVES):
+            picked = sb.tile([P, HALF], F32, name=f"kn_picked{h}")
+            nc.vector.tensor_copy(picked[:], kn_win[:].indirect(half_offsets(h)))
+            turned = ps.tile([P, BLOCKS, P], F32, name=f"kn_turned{h}")
+            for m in range(BLOCKS):
+                nc.tensor.transpose(turned[:, m, :], picked[:, m * P : (m + 1) * P], ident[:])
+            col = sb.tile([P, BLOCKS], F32, name=f"kn_col{h}")
+            nc.scalar.copy(col[:], turned[:, :, KN_ROW])
+            spread = ps.tile([P, BLOCKS, P], F32, name=f"kn_spread{h}")
+            for m in range(BLOCKS):
+                nc.tensor.transpose(spread[:, m, :], col[:, m : m + 1].to_broadcast([P, P]), ident[:])
+            both = sb.tile([P, HALF], F32, name=f"kq{h}")
+            nc.scalar.activation(both[:], spread[:].rearrange("p m s -> p (m s)"), ACT.Identity, bias=qn_col[:], scale=1.0)
+            kq.append(both)
+
+        k_planes = sb.tile([P, PASSES, N // 4], I32, name="k_planes", align_bytes=64)
+        nc.vector.memset(k_planes[:], 0)
+        scale_picked = sb.tile([P, PASSES, N], U8, name="scale_picked")
+        for o in range(PASSES):
+            nc.vector.tensor_copy(scale_picked[:, o, :], scale_win[:, o, :].bitcast(U8).indirect(offsets[:]))
+        for quad in range(4):
+            first = SC0 + 4 * SC_STEP * quad
+            nc.scalar.dma_start(
+                k_planes[32 * quad : 32 * quad + 4, :, :],
+                scale_picked[first : first + 4 * SC_STEP : SC_STEP, :, :].bitcast(I32),
+            )
+
+        q_codes, q_scales = [], []
+
+        def quantise_q(o):
+            grouped = sb.tile([P, NQ, 4], BF16, name=f"q_grouped{o}", align_bytes=64)
+            nc.scalar.copy(grouped[:], q_raw[o][:].rearrange("p j w -> p w j"))
+            codes = sb.tile([P, NQ], U32, name=f"q_codes{o}", align_bytes=64)
+            scales = sb.tile([P, NQ], U8, name=f"q_scales{o}", align_bytes=64)
+            nc.vector.quantize_mx(out=codes[:].bitcast(FP8X4), scales=scales[:], in_=grouped[:].rearrange("p w j -> p (w j)"))
+            q_codes.append(codes)
+            q_scales.append(scales)
+
+        def gather_words(h):
+            picked = sb.tile([P, HALF], U32, name=f"words_picked{h}")
+            nc.vector.tensor_copy(picked[:], word_win[:].bitcast(U32).indirect(half_offsets(h)))
+            return picked
+
+        def split_words(h, picked):
+            pairs = picked[:].bitcast(U16).rearrange("p (n o) -> p o n", o=PASSES)
+            parts = []
+            for o in range(PASSES):
+                part = sb.tile([P, HALF], U16, name=f"k_codes{h}_{o}", align_bytes=64)
+                nc.vector.tensor_copy(part[:], pairs[:, o, :])
+                parts.append(part)
+            return parts
+
+        picked0 = gather_words(0)
+        codes0 = split_words(0, picked0)
+        quantise_q(0)
+        picked1 = gather_words(1)
+        quantise_q(1)
+        codes1 = split_words(1, picked1)
+        k_codes = [codes0, codes1]
+
+        cells = HALF // SEG
+        for h in range(HALVES):
+            acc = ps.tile([P, HALF], F32, name=f"acc{h}")
+            for o in range(PASSES):
+                nc.tensor.matmul_mx(
+                    out=acc[:],
+                    lhsT=q_codes[o][:].bitcast(FP8X4),
+                    lhsT_scale=q_scales[o][:],
+                    rhs=k_codes[h][o][:].bitcast(FP4X4),
+                    rhs_scale=k_planes[:, o, :].bitcast(U8)[:, h * HALF : (h + 1) * HALF],
+                    start=(o == 0),
+                    stop=(o == PASSES - 1),
+                )
+            dist = sb.tile([P, HALF], F32, name=f"dist{h}")
+            nc.vector.scalar_tensor_tensor(dist[:], acc[:], -2.0, kq[h][:], ALU.mult, ALU.add)
+            least = sb.tile([P, cells], F32, name=f"least{h}")
+            nc.vector.tensor_reduce(least[:], dist[:].rearrange("p (c s) -> p c s", s=SEG), AXIS.X, ALU.min)
+            nc.sync.dma_start(out[0, :, h * cells : (h + 1) * cells], least[:])

@@ -32,23 +32,25 @@ def tile_attend_celldist_kernel(tc, qT, k_words, k_scales, kn, qn, offs, out):
     nc = tc.nc
     with ExitStack() as ctx:
         sb = ctx.enter_context(tc.tile_pool(name="sb", bufs=1))
+        shared = ctx.enter_context(tc.tile_pool(name="shared", bufs=1))
         ps = ctx.enter_context(tc.psum_pool(name="ps", bufs=1))
+        SCALE_AT, KN_AT, WORD_AT = 0, 8192, 24576
 
         offsets = sb.tile([P, N // 16], U16, name="offsets")
         nc.sync.dma_start(offsets[:], offs)
 
-        scale_win = sb.tile([P, PASSES, T // 4], I32, name="scale_win")
+        scale_win = shared.tile([P, PASSES, T // 4], I32, name="scale_win", offset=SCALE_AT, align_bytes=64)
         nc.vector.memset(scale_win[:], 0)
         nc.scalar.dma_start(
             scale_win[SC0 : SC0 + 16 * SC_STEP : SC_STEP, :, :],
             k_scales.rearrange("o f t -> f o t").bitcast(I32),
         )
-        kn_win = sb.tile([P, T], F32, name="kn_win")
+        kn_win = shared.tile([P, T], F32, name="kn_win", offset=KN_AT, align_bytes=64)
         nc.scalar.dma_start(kn_win[KN_ROW:P, :], kn[0:1, :])
         qn_col = sb.tile([P, 1], F32, name="qn_col")
         nc.scalar.dma_start(qn_col[:], qn[0])
 
-        word_win = sb.tile([P, T], I32, name="word_win")
+        word_win = shared.tile([P, T], I32, name="word_win", offset=WORD_AT, align_bytes=64)
         nc.sync.dma_start(word_win[:], k_words[0].rearrange("p t b -> p (t b)").bitcast(I32))
         q_raw = []
         for o in range(PASSES):
@@ -56,6 +58,8 @@ def tile_attend_celldist_kernel(tc, qT, k_words, k_scales, kn, qn, offs, out):
             nc.sync.dma_start(raw[:], qT[0, 512 * o : 512 * (o + 1), :].rearrange("(p j) w -> p j w", j=4))
             q_raw.append(raw)
 
+        k_planes = sb.tile([P, PASSES, N // 4], I32, name="k_planes", align_bytes=64)
+        nc.gpsimd.memset(k_planes[:], 0)
         ident = sb.tile([P, P], F32, name="ident")
         make_identity(nc, ident[:])
         nc.vector.memset(kn_win[0:KN_ROW, :], 0.0)
@@ -79,9 +83,7 @@ def tile_attend_celldist_kernel(tc, qT, k_words, k_scales, kn, qn, offs, out):
             nc.scalar.activation(both[:], spread[:].rearrange("p m s -> p (m s)"), ACT.Identity, bias=qn_col[:], scale=1.0)
             kq.append(both)
 
-        k_planes = sb.tile([P, PASSES, N // 4], I32, name="k_planes", align_bytes=64)
-        nc.vector.memset(k_planes[:], 0)
-        scale_picked = sb.tile([P, PASSES, N], U8, name="scale_picked")
+        scale_picked = shared.tile([P, PASSES, N], U8, name="scale_picked", offset=KN_AT, align_bytes=64)
         for o in range(PASSES):
             nc.vector.tensor_copy(scale_picked[:, o, :], scale_win[:, o, :].bitcast(U8).indirect(offsets[:]))
         for quad in range(4):
@@ -91,38 +93,29 @@ def tile_attend_celldist_kernel(tc, qT, k_words, k_scales, kn, qn, offs, out):
                 scale_picked[first : first + 4 * SC_STEP : SC_STEP, :, :].bitcast(I32),
             )
 
-        q_codes, q_scales = [], []
-
-        def quantise_q(o):
-            grouped = sb.tile([P, NQ, 4], BF16, name=f"q_grouped{o}", align_bytes=64)
+        q_grouped = []
+        for o in range(PASSES):
+            grouped = shared.tile([P, NQ, 4], BF16, name=f"q_grouped{o}", offset=SCALE_AT + 1024 * o, align_bytes=64)
             nc.scalar.copy(grouped[:], q_raw[o][:].rearrange("p j w -> p w j"))
-            codes = sb.tile([P, NQ], U32, name=f"q_codes{o}", align_bytes=64)
-            scales = sb.tile([P, NQ], U8, name=f"q_scales{o}", align_bytes=64)
-            nc.vector.quantize_mx(out=codes[:].bitcast(FP8X4), scales=scales[:], in_=grouped[:].rearrange("p w j -> p (w j)"))
-            q_codes.append(codes)
-            q_scales.append(scales)
+            q_grouped.append(grouped)
 
-        def gather_words(h):
-            picked = sb.tile([P, HALF], U32, name=f"words_picked{h}")
-            nc.vector.tensor_copy(picked[:], word_win[:].bitcast(U32).indirect(half_offsets(h)))
-            return picked
+        words_picked = shared.tile([P, N], U32, name="words_picked", offset=SCALE_AT + 2048, align_bytes=64)
+        nc.vector.tensor_copy(words_picked[:], word_win[:].bitcast(U32).indirect(offsets[:]))
+        pairs = words_picked[:].bitcast(U16).rearrange("p (n o) -> p o n", o=PASSES)
 
-        def split_words(h, picked):
-            pairs = picked[:].bitcast(U16).rearrange("p (n o) -> p o n", o=PASSES)
-            parts = []
+        q_codes, q_scales = [], []
+        k_codes = [[], []]
+        for h in range(HALVES):
             for o in range(PASSES):
                 part = sb.tile([P, HALF], U16, name=f"k_codes{h}_{o}", align_bytes=64)
-                nc.vector.tensor_copy(part[:], pairs[:, o, :])
-                parts.append(part)
-            return parts
-
-        picked0 = gather_words(0)
-        codes0 = split_words(0, picked0)
-        quantise_q(0)
-        picked1 = gather_words(1)
-        quantise_q(1)
-        codes1 = split_words(1, picked1)
-        k_codes = [codes0, codes1]
+                nc.vector.tensor_copy(part[:], pairs[:, o, h * HALF : (h + 1) * HALF])
+                k_codes[h].append(part)
+                if h == 0:
+                    codes = shared.tile([P, NQ], U32, name=f"q_codes{o}", offset=WORD_AT + 512 * o, align_bytes=64)
+                    scales = sb.tile([P, NQ], U8, name=f"q_scales{o}", align_bytes=64)
+                    nc.vector.quantize_mx(out=codes[:].bitcast(FP8X4), scales=scales[:], in_=q_grouped[o][:].rearrange("p w j -> p (w j)"))
+                    q_codes.append(codes)
+                    q_scales.append(scales)
 
         cells = HALF // SEG
         for h in range(HALVES):

@@ -21,11 +21,18 @@ PASSES = D // 512
 HALF = 512
 HALVES = N // HALF
 BLOCKS = HALF // P
+PIECE = 256
 KN_ROW = P - 1
-SC0, SC_STEP = 32, 4
+SC_STEP = 4
 
 FLOPS = 2 * NQ * N * D
 BYTES = 4 * D * NQ + 4 * P * T + 2 * 16 * T + 4 * T + 4 * NQ + 2 * P * (N // 16) + 4 * NQ * (N // SEG)
+
+SCALE_AT = 0
+KN_PICKED_AT = 0
+KN_AT = 4096
+WORDS_PICKED_AT = KN_AT
+WORD_AT = KN_AT + 4 * T
 
 
 def tile_attend_celldist_kernel(tc, qT, k_words, k_scales, kn, qn, offs, out):
@@ -34,17 +41,13 @@ def tile_attend_celldist_kernel(tc, qT, k_words, k_scales, kn, qn, offs, out):
         sb = ctx.enter_context(tc.tile_pool(name="sb", bufs=1))
         shared = ctx.enter_context(tc.tile_pool(name="shared", bufs=1))
         ps = ctx.enter_context(tc.psum_pool(name="ps", bufs=1))
-        SCALE_AT, KN_AT, WORD_AT = 0, 8192, 24576
 
         offsets = sb.tile([P, N // 16], U16, name="offsets")
         nc.sync.dma_start(offsets[:], offs)
 
-        scale_win = shared.tile([P, PASSES, T // 4], I32, name="scale_win", offset=SCALE_AT, align_bytes=64)
+        scale_win = shared.tile([P, T // 4], I32, name="scale_win", offset=SCALE_AT, align_bytes=64)
         nc.vector.memset(scale_win[:], 0)
-        nc.scalar.dma_start(
-            scale_win[SC0 : SC0 + 16 * SC_STEP : SC_STEP, :, :],
-            k_scales.rearrange("o f t -> f o t").bitcast(I32),
-        )
+        nc.scalar.dma_start(scale_win[0:P:SC_STEP, :], k_scales.rearrange("o f t -> (o f) t").bitcast(I32))
         kn_win = shared.tile([P, T], F32, name="kn_win", offset=KN_AT, align_bytes=64)
         nc.scalar.dma_start(kn_win[KN_ROW:P, :], kn[0:1, :])
         qn_col = sb.tile([P, 1], F32, name="qn_col")
@@ -60,16 +63,15 @@ def tile_attend_celldist_kernel(tc, qT, k_words, k_scales, kn, qn, offs, out):
 
         k_planes = sb.tile([P, PASSES, N // 4], I32, name="k_planes", align_bytes=64)
         nc.gpsimd.memset(k_planes[:], 0)
-        ident = sb.tile([P, P], F32, name="ident")
-        make_identity(nc, ident[:])
         nc.vector.memset(kn_win[0:KN_ROW, :], 0.0)
+        ident = sb.tile([P, P], F32, name="ident")
+        nc.vector.memset(ident[:], 0.0)
+        make_identity(nc, ident[:], nomemset=True)
 
         def half_offsets(h):
             return offsets[:, h * (HALF // 16) : (h + 1) * (HALF // 16)]
 
-        kq = []
-        for h in range(HALVES):
-            picked = sb.tile([P, HALF], F32, name=f"kn_picked{h}")
+        def spread_norms(h, picked):
             nc.vector.tensor_copy(picked[:], kn_win[:].indirect(half_offsets(h)))
             turned = ps.tile([P, BLOCKS, P], F32, name=f"kn_turned{h}")
             for m in range(BLOCKS):
@@ -81,26 +83,37 @@ def tile_attend_celldist_kernel(tc, qT, k_words, k_scales, kn, qn, offs, out):
                 nc.tensor.transpose(spread[:, m, :], col[:, m : m + 1].to_broadcast([P, P]), ident[:])
             both = sb.tile([P, HALF], F32, name=f"kq{h}")
             nc.scalar.activation(both[:], spread[:].rearrange("p m s -> p (m s)"), ACT.Identity, bias=qn_col[:], scale=1.0)
-            kq.append(both)
+            return both
 
-        scale_picked = shared.tile([P, PASSES, N], U8, name="scale_picked", offset=KN_AT, align_bytes=64)
+        kn_picked0 = sb.tile([P, HALF], F32, name="kn_picked0")
+        kq = [spread_norms(0, kn_picked0)]
+
+        scale_picked = sb.tile([P, N], U8, name="scale_picked")
+        nc.vector.tensor_copy(scale_picked[:], scale_win[:].bitcast(U8).indirect(offsets[:]))
         for o in range(PASSES):
-            nc.vector.tensor_copy(scale_picked[:, o, :], scale_win[:, o, :].bitcast(U8).indirect(offsets[:]))
-        for quad in range(4):
-            first = SC0 + 4 * SC_STEP * quad
-            nc.scalar.dma_start(
-                k_planes[32 * quad : 32 * quad + 4, :, :],
-                scale_picked[first : first + 4 * SC_STEP : SC_STEP, :, :].bitcast(I32),
-            )
+            for quad in range(4):
+                first = SC_STEP * (16 * o + 4 * quad)
+                nc.sync.dma_start(
+                    k_planes[32 * quad : 32 * quad + 4, o, :],
+                    scale_picked[first : first + 4 * SC_STEP : SC_STEP, :].bitcast(I32),
+                )
+
+        kn_picked1 = shared.tile([P, HALF], F32, name="kn_picked1", offset=KN_PICKED_AT, align_bytes=64)
+        kq.append(spread_norms(1, kn_picked1))
 
         q_grouped = []
         for o in range(PASSES):
-            grouped = shared.tile([P, NQ, 4], BF16, name=f"q_grouped{o}", offset=SCALE_AT + 1024 * o, align_bytes=64)
+            grouped = shared.tile(
+                [P, NQ, 4], BF16, name=f"q_grouped{o}", offset=KN_PICKED_AT + 1024 * o, align_bytes=64
+            )
             nc.scalar.copy(grouped[:], q_raw[o][:].rearrange("p j w -> p w j"))
             q_grouped.append(grouped)
 
-        words_picked = shared.tile([P, N], U32, name="words_picked", offset=SCALE_AT + 2048, align_bytes=64)
-        nc.vector.tensor_copy(words_picked[:], word_win[:].bitcast(U32).indirect(offsets[:]))
+        words_picked = shared.tile([P, N], U32, name="words_picked", offset=WORDS_PICKED_AT, align_bytes=64)
+        for h in range(HALVES):
+            nc.vector.tensor_copy(
+                words_picked[:, h * HALF : (h + 1) * HALF], word_win[:].bitcast(U32).indirect(half_offsets(h))
+            )
         pairs = words_picked[:].bitcast(U16).rearrange("p (n o) -> p o n", o=PASSES)
 
         q_codes, q_scales = [], []
@@ -113,7 +126,9 @@ def tile_attend_celldist_kernel(tc, qT, k_words, k_scales, kn, qn, offs, out):
                 if h == 0:
                     codes = shared.tile([P, NQ], U32, name=f"q_codes{o}", offset=WORD_AT + 512 * o, align_bytes=64)
                     scales = sb.tile([P, NQ], U8, name=f"q_scales{o}", align_bytes=64)
-                    nc.vector.quantize_mx(out=codes[:].bitcast(FP8X4), scales=scales[:], in_=q_grouped[o][:].rearrange("p w j -> p (w j)"))
+                    nc.vector.quantize_mx(
+                        out=codes[:].bitcast(FP8X4), scales=scales[:], in_=q_grouped[o][:].rearrange("p w j -> p (w j)")
+                    )
                     q_codes.append(codes)
                     q_scales.append(scales)
 
@@ -131,7 +146,15 @@ def tile_attend_celldist_kernel(tc, qT, k_words, k_scales, kn, qn, offs, out):
                     stop=(o == PASSES - 1),
                 )
             dist = sb.tile([P, HALF], F32, name=f"dist{h}")
-            nc.vector.scalar_tensor_tensor(dist[:], acc[:], -2.0, kq[h][:], ALU.mult, ALU.add)
             least = sb.tile([P, cells], F32, name=f"least{h}")
-            nc.vector.tensor_reduce(least[:], dist[:].rearrange("p (c s) -> p c s", s=SEG), AXIS.X, ALU.min)
+            pieces = [slice(c, c + PIECE) for c in range(0, HALF, PIECE)]
+            for cols in pieces:
+                nc.vector.scalar_tensor_tensor(dist[:, cols], acc[:, cols], -2.0, kq[h][:, cols], ALU.mult, ALU.add)
+            for cols in pieces:
+                nc.vector.tensor_reduce(
+                    least[:, cols.start // SEG : cols.stop // SEG],
+                    dist[:, cols].rearrange("p (c s) -> p c s", s=SEG),
+                    AXIS.X,
+                    ALU.min,
+                )
             nc.sync.dma_start(out[0, :, h * cells : (h + 1) * cells], least[:])

@@ -29,10 +29,12 @@ FLOPS = 2 * NQ * N * D
 BYTES = 4 * D * NQ + 4 * P * T + 2 * 16 * T + 4 * T + 4 * NQ + 2 * P * (N // 16) + 4 * NQ * (N // SEG)
 
 SCALE_AT = 0
-KN_PICKED_AT = 0
-KN_AT = 4096
-WORDS_PICKED_AT = KN_AT
+PLANES_AT = 0
+KN_PICKED_AT = 3072
+KN_AT = 8192
 WORD_AT = KN_AT + 4 * T
+GROUPED_AT = WORD_AT + 4 * T
+RAW_AT = GROUPED_AT + 4096
 
 
 def tile_attend_celldist_kernel(tc, qT, k_words, k_scales, kn, qn, offs, out):
@@ -42,27 +44,26 @@ def tile_attend_celldist_kernel(tc, qT, k_words, k_scales, kn, qn, offs, out):
         shared = ctx.enter_context(tc.tile_pool(name="shared", bufs=1))
         ps = ctx.enter_context(tc.psum_pool(name="ps", bufs=1))
 
+        def at(offset, shape, dtype, name):
+            return shared.tile(shape, dtype, name=name, offset=offset, align_bytes=64)
+
         offsets = sb.tile([P, N // 16], U16, name="offsets")
         nc.sync.dma_start(offsets[:], offs)
-
-        scale_win = shared.tile([P, T // 4], I32, name="scale_win", offset=SCALE_AT, align_bytes=64)
-        nc.vector.memset(scale_win[:], 0)
-        nc.scalar.dma_start(scale_win[0:P:SC_STEP, :], k_scales.rearrange("o f t -> (o f) t").bitcast(I32))
-        kn_win = shared.tile([P, T], F32, name="kn_win", offset=KN_AT, align_bytes=64)
+        kn_win = at(KN_AT, [P, T], F32, "kn_win")
         nc.scalar.dma_start(kn_win[KN_ROW:P, :], kn[0:1, :])
         qn_col = sb.tile([P, 1], F32, name="qn_col")
         nc.scalar.dma_start(qn_col[:], qn[0])
-
-        word_win = shared.tile([P, T], I32, name="word_win", offset=WORD_AT, align_bytes=64)
+        word_win = at(WORD_AT, [P, T], I32, "word_win")
         nc.sync.dma_start(word_win[:], k_words[0].rearrange("p t b -> p (t b)").bitcast(I32))
         q_raw = []
         for o in range(PASSES):
-            raw = sb.tile([P, 4, NQ], F32, name=f"q_raw{o}")
+            raw = at(RAW_AT + 2048 * o, [P, 4, NQ], F32, f"q_raw{o}")
             nc.sync.dma_start(raw[:], qT[0, 512 * o : 512 * (o + 1), :].rearrange("(p j) w -> p j w", j=4))
             q_raw.append(raw)
 
-        k_planes = sb.tile([P, PASSES, N // 4], I32, name="k_planes", align_bytes=64)
-        nc.gpsimd.memset(k_planes[:], 0)
+        scale_win = at(SCALE_AT, [P, T // 4], I32, "scale_win")
+        nc.vector.memset(scale_win[:], 0)
+        nc.scalar.dma_start(scale_win[0:P:SC_STEP, :], k_scales.bitcast(I32).rearrange("o f t -> f o t"))
         nc.vector.memset(kn_win[0:KN_ROW, :], 0.0)
         ident = sb.tile([P, P], F32, name="ident")
         nc.vector.memset(ident[:], 0.0)
@@ -81,56 +82,63 @@ def tile_attend_celldist_kernel(tc, qT, k_words, k_scales, kn, qn, offs, out):
             spread = ps.tile([P, BLOCKS, P], F32, name=f"kn_spread{h}")
             for m in range(BLOCKS):
                 nc.tensor.transpose(spread[:, m, :], col[:, m : m + 1].to_broadcast([P, P]), ident[:])
-            both = sb.tile([P, HALF], F32, name=f"kq{h}")
-            nc.scalar.activation(both[:], spread[:].rearrange("p m s -> p (m s)"), ACT.Identity, bias=qn_col[:], scale=1.0)
-            return both
+            return spread
 
-        kn_picked0 = sb.tile([P, HALF], F32, name="kn_picked0")
-        kq = [spread_norms(0, kn_picked0)]
-
-        scale_picked = sb.tile([P, N], U8, name="scale_picked")
+        spreads = [spread_norms(0, sb.tile([P, HALF], F32, name="kn_picked0"))]
+        scale_picked = at(GROUPED_AT + 1536, [P, N], U8, "scale_picked")
         nc.vector.tensor_copy(scale_picked[:], scale_win[:].bitcast(U8).indirect(offsets[:]))
-        for o in range(PASSES):
-            for quad in range(4):
-                first = SC_STEP * (16 * o + 4 * quad)
-                nc.sync.dma_start(
-                    k_planes[32 * quad : 32 * quad + 4, o, :],
-                    scale_picked[first : first + 4 * SC_STEP : SC_STEP, :].bitcast(I32),
-                )
-
-        kn_picked1 = shared.tile([P, HALF], F32, name="kn_picked1", offset=KN_PICKED_AT, align_bytes=64)
-        kq.append(spread_norms(1, kn_picked1))
+        k_planes = at(PLANES_AT, [P, PASSES * N // 4], I32, "k_planes")
+        for quad in range(4):
+            nc.scalar.dma_start(
+                k_planes[32 * quad : 32 * quad + 4, :],
+                scale_picked[32 * quad : 32 * quad + 32 : SC_STEP, :].bitcast(I32),
+            )
+        spreads.append(spread_norms(1, at(KN_PICKED_AT, [P, HALF], F32, "kn_picked1")))
 
         q_grouped = []
         for o in range(PASSES):
-            grouped = shared.tile(
-                [P, NQ, 4], BF16, name=f"q_grouped{o}", offset=KN_PICKED_AT + 1024 * o, align_bytes=64
-            )
+            grouped = at(GROUPED_AT + 1024 * (o + 1), [P, NQ, 4], BF16, f"q_grouped{o}")
             nc.scalar.copy(grouped[:], q_raw[o][:].rearrange("p j w -> p w j"))
             q_grouped.append(grouped)
-
-        words_picked = shared.tile([P, N], U32, name="words_picked", offset=WORDS_PICKED_AT, align_bytes=64)
+        kq = []
         for h in range(HALVES):
-            nc.vector.tensor_copy(
-                words_picked[:, h * HALF : (h + 1) * HALF], word_win[:].bitcast(U32).indirect(half_offsets(h))
+            both = at(RAW_AT + 2048 * (1 - h), [P, HALF], F32, f"kq{h}")
+            nc.scalar.activation(
+                both[:], spreads[h][:].rearrange("p m s -> p (m s)"), ACT.Identity, bias=qn_col[:], scale=1.0
             )
-        pairs = words_picked[:].bitcast(U16).rearrange("p (n o) -> p o n", o=PASSES)
+            kq.append(both)
 
         q_codes, q_scales = [], []
         k_codes = [[], []]
+        picked_at = [KN_AT, GROUPED_AT]
+        codes_at = [KN_AT + 4096, WORD_AT]
+        parts_at = [KN_AT + 8192, GROUPED_AT + 2048]
         for h in range(HALVES):
-            for o in range(PASSES):
-                part = sb.tile([P, HALF], U16, name=f"k_codes{h}_{o}", align_bytes=64)
-                nc.vector.tensor_copy(part[:], pairs[:, o, h * HALF : (h + 1) * HALF])
-                k_codes[h].append(part)
-                if h == 0:
-                    codes = shared.tile([P, NQ], U32, name=f"q_codes{o}", offset=WORD_AT + 512 * o, align_bytes=64)
-                    scales = sb.tile([P, NQ], U8, name=f"q_scales{o}", align_bytes=64)
-                    nc.vector.quantize_mx(
-                        out=codes[:].bitcast(FP8X4), scales=scales[:], in_=q_grouped[o][:].rearrange("p w j -> p (w j)")
-                    )
-                    q_codes.append(codes)
-                    q_scales.append(scales)
+            words_picked = at(picked_at[h], [P, HALF], U32, f"words_picked{h}")
+            nc.vector.tensor_copy(words_picked[:], word_win[:].bitcast(U32).indirect(half_offsets(h)))
+            pairs = words_picked[:].bitcast(U16).rearrange("p (n o) -> p o n", o=PASSES)
+
+            def part_words():
+                for o in range(PASSES):
+                    part = at(parts_at[h] + 1024 * o, [P, HALF], U16, f"k_codes{h}_{o}")
+                    nc.vector.tensor_copy(part[:], pairs[:, o, :])
+                    k_codes[h].append(part)
+
+            def quantize(o):
+                codes = at(codes_at[o], [P, NQ], U32, f"q_codes{o}")
+                scales = sb.tile([P, NQ], U8, name=f"q_scales{o}", align_bytes=64)
+                nc.vector.quantize_mx(
+                    out=codes[:].bitcast(FP8X4), scales=scales[:], in_=q_grouped[o][:].rearrange("p w j -> p (w j)")
+                )
+                q_codes.append(codes)
+                q_scales.append(scales)
+
+            if h == 0:
+                part_words()
+                quantize(h)
+            else:
+                quantize(h)
+                part_words()
 
         cells = HALF // SEG
         for h in range(HALVES):
@@ -141,7 +149,7 @@ def tile_attend_celldist_kernel(tc, qT, k_words, k_scales, kn, qn, offs, out):
                     lhsT=q_codes[o][:].bitcast(FP8X4),
                     lhsT_scale=q_scales[o][:],
                     rhs=k_codes[h][o][:].bitcast(FP4X4),
-                    rhs_scale=k_planes[:, o, :].bitcast(U8)[:, h * HALF : (h + 1) * HALF],
+                    rhs_scale=k_planes[:].bitcast(U8)[:, o * N + h * HALF : o * N + (h + 1) * HALF],
                     start=(o == 0),
                     stop=(o == PASSES - 1),
                 )

@@ -23,18 +23,17 @@ HALVES = N // HALF
 BLOCKS = HALF // P
 PIECE = 256
 KN_ROW = P - 1
-SC_STEP = 4
+SC_FIRST = P - 32
 
 FLOPS = 2 * NQ * N * D
 BYTES = 4 * D * NQ + 4 * P * T + 2 * 16 * T + 4 * T + 4 * NQ + 2 * P * (N // 16) + 4 * NQ * (N // SEG)
 
 SCALE_AT = 0
-PLANES_AT = 0
-KN_PICKED_AT = 3072
-KN_AT = 8192
+KN_AT = 4096
 WORD_AT = KN_AT + 4 * T
 GROUPED_AT = WORD_AT + 4 * T
 RAW_AT = GROUPED_AT + 4096
+KN_PICKED_AT = RAW_AT + 6144
 
 
 def tile_attend_celldist_kernel(tc, qT, k_words, k_scales, kn, qn, offs, out):
@@ -51,6 +50,8 @@ def tile_attend_celldist_kernel(tc, qT, k_words, k_scales, kn, qn, offs, out):
         nc.sync.dma_start(offsets[:], offs)
         kn_win = at(KN_AT, [P, T], F32, "kn_win")
         nc.scalar.dma_start(kn_win[KN_ROW:P, :], kn[0:1, :])
+        scale_win = at(SCALE_AT, [P, T // 4], I32, "scale_win")
+        nc.sync.dma_start(scale_win[SC_FIRST:P, :], k_scales.bitcast(I32).rearrange("o f t -> f o t"))
         qn_col = sb.tile([P, 1], F32, name="qn_col")
         nc.scalar.dma_start(qn_col[:], qn[0])
         word_win = at(WORD_AT, [P, T], I32, "word_win")
@@ -61,9 +62,7 @@ def tile_attend_celldist_kernel(tc, qT, k_words, k_scales, kn, qn, offs, out):
             nc.sync.dma_start(raw[:], qT[0, 512 * o : 512 * (o + 1), :].rearrange("(p j) w -> p j w", j=4))
             q_raw.append(raw)
 
-        scale_win = at(SCALE_AT, [P, T // 4], I32, "scale_win")
-        nc.vector.memset(scale_win[:], 0)
-        nc.scalar.dma_start(scale_win[0:P:SC_STEP, :], k_scales.bitcast(I32).rearrange("o f t -> f o t"))
+        nc.vector.memset(scale_win[0:SC_FIRST, :], 0)
         nc.vector.memset(kn_win[0:KN_ROW, :], 0.0)
         ident = sb.tile([P, P], F32, name="ident")
         nc.vector.memset(ident[:], 0.0)
@@ -84,16 +83,21 @@ def tile_attend_celldist_kernel(tc, qT, k_words, k_scales, kn, qn, offs, out):
                 nc.tensor.transpose(spread[:, m, :], col[:, m : m + 1].to_broadcast([P, P]), ident[:])
             return spread
 
-        spreads = [spread_norms(0, sb.tile([P, HALF], F32, name="kn_picked0"))]
-        scale_picked = at(GROUPED_AT + 1536, [P, N], U8, "scale_picked")
-        nc.vector.tensor_copy(scale_picked[:], scale_win[:].bitcast(U8).indirect(offsets[:]))
-        k_planes = at(PLANES_AT, [P, PASSES * N // 4], I32, "k_planes")
-        for quad in range(4):
-            nc.scalar.dma_start(
-                k_planes[32 * quad : 32 * quad + 4, :],
-                scale_picked[32 * quad : 32 * quad + 32 : SC_STEP, :].bitcast(I32),
-            )
-        spreads.append(spread_norms(1, at(KN_PICKED_AT, [P, HALF], F32, "kn_picked1")))
+        def gather_planes(h, picked, planes, queue):
+            nc.vector.tensor_copy(picked[:], scale_win[:].bitcast(U8).indirect(half_offsets(h)))
+            for quad in range(4):
+                first = SC_FIRST + 8 * quad
+                queue.dma_start(planes[32 * quad : 32 * quad + 4, :], picked[first : first + 8, :].bitcast(I32))
+
+        spreads, k_planes = [], []
+        norms_at = [KN_PICKED_AT, GROUPED_AT + 1024]
+        planes_at = [KN_PICKED_AT, SCALE_AT + 2048]
+        scales_at = [KN_PICKED_AT + 2048, KN_AT]
+        queues = [nc.scalar, nc.sync]
+        for h in range(HALVES):
+            spreads.append(spread_norms(h, at(norms_at[h], [P, HALF], F32, f"kn_picked{h}")))
+            k_planes.append(at(planes_at[h], [P, PASSES * HALF // 4], I32, f"k_planes{h}"))
+            gather_planes(h, at(scales_at[h], [P, HALF], U8, f"scale_picked{h}"), k_planes[h], queues[h])
 
         q_grouped = []
         for o in range(PASSES):
@@ -102,7 +106,7 @@ def tile_attend_celldist_kernel(tc, qT, k_words, k_scales, kn, qn, offs, out):
             q_grouped.append(grouped)
         kq = []
         for h in range(HALVES):
-            both = at(RAW_AT + 2048 * (1 - h), [P, HALF], F32, f"kq{h}")
+            both = at(RAW_AT + 2048 * h, [P, HALF], F32, f"kq{h}")
             nc.scalar.activation(
                 both[:], spreads[h][:].rearrange("p m s -> p (m s)"), ACT.Identity, bias=qn_col[:], scale=1.0
             )
@@ -110,7 +114,7 @@ def tile_attend_celldist_kernel(tc, qT, k_words, k_scales, kn, qn, offs, out):
 
         q_codes, q_scales = [], []
         k_codes = [[], []]
-        picked_at = [KN_AT, GROUPED_AT]
+        picked_at = [SCALE_AT, GROUPED_AT]
         codes_at = [KN_AT + 4096, WORD_AT]
         parts_at = [KN_AT + 8192, GROUPED_AT + 2048]
         for h in range(HALVES):
@@ -149,7 +153,7 @@ def tile_attend_celldist_kernel(tc, qT, k_words, k_scales, kn, qn, offs, out):
                     lhsT=q_codes[o][:].bitcast(FP8X4),
                     lhsT_scale=q_scales[o][:],
                     rhs=k_codes[h][o][:].bitcast(FP4X4),
-                    rhs_scale=k_planes[:].bitcast(U8)[:, o * N + h * HALF : o * N + (h + 1) * HALF],
+                    rhs_scale=k_planes[h][:].bitcast(U8)[:, o * HALF : (o + 1) * HALF],
                     start=(o == 0),
                     stop=(o == PASSES - 1),
                 )

@@ -23,7 +23,7 @@ HALVES = N // HALF
 BLOCKS = HALF // P
 PIECE = 256
 KN_ROW = P - 1
-SC_FIRST = P - 32
+SC_ROWS = 32
 
 FLOPS = 2 * NQ * N * D
 BYTES = 4 * D * NQ + 4 * P * T + 2 * 16 * T + 4 * T + 4 * NQ + 2 * P * (N // 16) + 4 * NQ * (N // SEG)
@@ -51,7 +51,7 @@ def tile_attend_celldist_kernel(tc, qT, k_words, k_scales, kn, qn, offs, out):
         kn_win = at(KN_AT, [P, T], F32, "kn_win")
         nc.scalar.dma_start(kn_win[KN_ROW:P, :], kn[0:1, :])
         scale_win = at(SCALE_AT, [P, T // 4], I32, "scale_win")
-        nc.sync.dma_start(scale_win[SC_FIRST:P, :], k_scales.bitcast(I32).rearrange("o f t -> f o t"))
+        nc.sync.dma_start(scale_win[0:SC_ROWS, :], k_scales.bitcast(I32).rearrange("o f t -> f o t"))
         qn_col = sb.tile([P, 1], F32, name="qn_col")
         nc.scalar.dma_start(qn_col[:], qn[0])
         word_win = at(WORD_AT, [P, T], I32, "word_win")
@@ -62,7 +62,8 @@ def tile_attend_celldist_kernel(tc, qT, k_words, k_scales, kn, qn, offs, out):
             nc.sync.dma_start(raw[:], qT[0, 512 * o : 512 * (o + 1), :].rearrange("(p j) w -> p j w", j=4))
             q_raw.append(raw)
 
-        nc.vector.memset(scale_win[0:SC_FIRST, :], 0)
+        nc.vector.memset(scale_win[SC_ROWS:64, :], 0)
+        nc.vector.memset(scale_win[64:P, :], 0)
         nc.vector.memset(kn_win[0:KN_ROW, :], 0.0)
         ident = sb.tile([P, P], F32, name="ident")
         nc.vector.memset(ident[:], 0.0)
@@ -86,7 +87,7 @@ def tile_attend_celldist_kernel(tc, qT, k_words, k_scales, kn, qn, offs, out):
         def gather_planes(h, picked, planes, queue):
             nc.vector.tensor_copy(picked[:], scale_win[:].bitcast(U8).indirect(half_offsets(h)))
             for quad in range(4):
-                first = SC_FIRST + 8 * quad
+                first = 8 * quad
                 queue.dma_start(planes[32 * quad : 32 * quad + 4, :], picked[first : first + 8, :].bitcast(I32))
 
         spreads, k_planes = [], []

@@ -28,12 +28,12 @@ SC_ROWS = 32
 FLOPS = 2 * NQ * N * D
 BYTES = 4 * D * NQ + 4 * P * T + 2 * 16 * T + 4 * T + 4 * NQ + 2 * P * (N // 16) + 4 * NQ * (N // SEG)
 
+SC_FIRST = P - SC_ROWS
 SCALE_AT = 0
-KN_AT = 4096
-WORD_AT = KN_AT + 4 * T
-GROUPED_AT = WORD_AT + 4 * T
-RAW_AT = GROUPED_AT + 4096
-KN_PICKED_AT = RAW_AT + 6144
+RAW_AT = [4096, 8192]
+PART_AT = [[RAW_AT[0], RAW_AT[1] - 512], [RAW_AT[1] + 512, RAW_AT[1] + 1536]]
+KN_PICKED_AT = [14336, 20480]
+WORDS_PICKED_AT = [KN_PICKED_AT[0] - 1024, KN_PICKED_AT[0] + 1024]
 
 
 def tile_attend_celldist_kernel(tc, qT, k_words, k_scales, kn, qn, offs, out):
@@ -48,22 +48,21 @@ def tile_attend_celldist_kernel(tc, qT, k_words, k_scales, kn, qn, offs, out):
 
         offsets = sb.tile([P, N // 16], U16, name="offsets")
         nc.sync.dma_start(offsets[:], offs)
-        kn_win = at(KN_AT, [P, T], F32, "kn_win")
+        kn_win = sb.tile([P, T], F32, name="kn_win")
         nc.scalar.dma_start(kn_win[KN_ROW:P, :], kn[0:1, :])
         scale_win = at(SCALE_AT, [P, T // 4], I32, "scale_win")
-        nc.sync.dma_start(scale_win[0:SC_ROWS, :], k_scales.bitcast(I32).rearrange("o f t -> f o t"))
-        qn_col = sb.tile([P, 1], F32, name="qn_col")
-        nc.scalar.dma_start(qn_col[:], qn[0])
-        word_win = at(WORD_AT, [P, T], I32, "word_win")
+        nc.scalar.dma_start(scale_win[SC_FIRST:P, :], k_scales.bitcast(I32).rearrange("o f t -> f o t"))
+        word_win = sb.tile([P, T], I32, name="word_win")
         nc.sync.dma_start(word_win[:], k_words[0].rearrange("p t b -> p (t b)").bitcast(I32))
         q_raw = []
         for o in range(PASSES):
-            raw = at(RAW_AT + 2048 * o, [P, 4, NQ], F32, f"q_raw{o}")
+            raw = at(RAW_AT[o], [P, 4, NQ], F32, f"q_raw{o}")
             nc.sync.dma_start(raw[:], qT[0, 512 * o : 512 * (o + 1), :].rearrange("(p j) w -> p j w", j=4))
             q_raw.append(raw)
+        qn_col = sb.tile([P, 1], F32, name="qn_col")
+        nc.sync.dma_start(qn_col[:], qn[0])
 
-        nc.vector.memset(scale_win[SC_ROWS:64, :], 0)
-        nc.vector.memset(scale_win[64:P, :], 0)
+        nc.vector.memset(scale_win[0:SC_FIRST, :], 0)
         nc.vector.memset(kn_win[0:KN_ROW, :], 0.0)
         ident = sb.tile([P, P], F32, name="ident")
         nc.vector.memset(ident[:], 0.0)
@@ -72,7 +71,8 @@ def tile_attend_celldist_kernel(tc, qT, k_words, k_scales, kn, qn, offs, out):
         def half_offsets(h):
             return offsets[:, h * (HALF // 16) : (h + 1) * (HALF // 16)]
 
-        def spread_norms(h, picked):
+        def spread_norms(h):
+            picked = at(KN_PICKED_AT[h], [P, HALF], F32, f"kn_picked{h}")
             nc.vector.tensor_copy(picked[:], kn_win[:].indirect(half_offsets(h)))
             turned = ps.tile([P, BLOCKS, P], F32, name=f"kn_turned{h}")
             for m in range(BLOCKS):
@@ -84,77 +84,64 @@ def tile_attend_celldist_kernel(tc, qT, k_words, k_scales, kn, qn, offs, out):
                 nc.tensor.transpose(spread[:, m, :], col[:, m : m + 1].to_broadcast([P, P]), ident[:])
             return spread
 
-        def gather_planes(h, picked, planes, queue):
-            nc.vector.tensor_copy(picked[:], scale_win[:].bitcast(U8).indirect(half_offsets(h)))
-            for quad in range(4):
-                first = 8 * quad
-                queue.dma_start(planes[32 * quad : 32 * quad + 4, :], picked[first : first + 8, :].bitcast(I32))
-
-        spreads, k_planes = [], []
-        norms_at = [KN_PICKED_AT, GROUPED_AT + 1024]
-        planes_at = [KN_PICKED_AT, SCALE_AT + 2048]
-        scales_at = [KN_PICKED_AT + 2048, KN_AT]
-        queues = [nc.scalar, nc.sync]
-        for h in range(HALVES):
-            spreads.append(spread_norms(h, at(norms_at[h], [P, HALF], F32, f"kn_picked{h}")))
-            k_planes.append(at(planes_at[h], [P, PASSES * HALF // 4], I32, f"k_planes{h}"))
-            gather_planes(h, at(scales_at[h], [P, HALF], U8, f"scale_picked{h}"), k_planes[h], queues[h])
+        spreads = [spread_norms(0)]
+        scale_picked = sb.tile([P, N], U8, name="scale_picked")
+        nc.vector.tensor_copy(scale_picked[:], scale_win[:].bitcast(U8).indirect(offsets[:]))
+        k_planes = at(SCALE_AT, [P, PASSES * N // 4], I32, "k_planes")
+        for quad in range(4):
+            first = SC_FIRST + 8 * quad
+            nc.scalar.dma_start(k_planes[32 * quad : 32 * quad + 4, :], scale_picked[first : first + 8, :].bitcast(I32))
+        spreads.append(spread_norms(1))
 
         q_grouped = []
         for o in range(PASSES):
-            grouped = at(GROUPED_AT + 1024 * (o + 1), [P, NQ, 4], BF16, f"q_grouped{o}")
+            grouped = sb.tile([P, NQ, 4], BF16, name=f"q_grouped{o}", align_bytes=64)
             nc.scalar.copy(grouped[:], q_raw[o][:].rearrange("p j w -> p w j"))
             q_grouped.append(grouped)
         kq = []
         for h in range(HALVES):
-            both = at(RAW_AT + 2048 * h, [P, HALF], F32, f"kq{h}")
+            both = sb.tile([P, HALF], F32, name=f"kq{h}")
             nc.scalar.activation(
                 both[:], spreads[h][:].rearrange("p m s -> p (m s)"), ACT.Identity, bias=qn_col[:], scale=1.0
             )
             kq.append(both)
 
+        pairs = []
+        for h in range(HALVES):
+            words_picked = at(WORDS_PICKED_AT[h], [P, HALF], U32, f"words_picked{h}")
+            nc.vector.tensor_copy(words_picked[:], word_win[:].bitcast(U32).indirect(half_offsets(h)))
+            pairs.append(words_picked[:].bitcast(U16).rearrange("p (n o) -> p o n", o=PASSES))
+
+        def part_words(h, o):
+            part = at(PART_AT[h][o], [P, HALF], U16, f"k_codes{h}_{o}")
+            nc.vector.tensor_copy(part[:], pairs[h][:, o, :])
+            return part
+
         q_codes, q_scales = [], []
         k_codes = [[], []]
-        picked_at = [SCALE_AT, GROUPED_AT]
-        codes_at = [KN_AT + 4096, WORD_AT]
-        parts_at = [KN_AT + 8192, GROUPED_AT + 2048]
-        for h in range(HALVES):
-            words_picked = at(picked_at[h], [P, HALF], U32, f"words_picked{h}")
-            nc.vector.tensor_copy(words_picked[:], word_win[:].bitcast(U32).indirect(half_offsets(h)))
-            pairs = words_picked[:].bitcast(U16).rearrange("p (n o) -> p o n", o=PASSES)
-
-            def part_words():
-                for o in range(PASSES):
-                    part = at(parts_at[h] + 1024 * o, [P, HALF], U16, f"k_codes{h}_{o}")
-                    nc.vector.tensor_copy(part[:], pairs[:, o, :])
-                    k_codes[h].append(part)
-
-            def quantize(o):
-                codes = at(codes_at[o], [P, NQ], U32, f"q_codes{o}")
-                scales = sb.tile([P, NQ], U8, name=f"q_scales{o}", align_bytes=64)
-                nc.vector.quantize_mx(
-                    out=codes[:].bitcast(FP8X4), scales=scales[:], in_=q_grouped[o][:].rearrange("p w j -> p (w j)")
-                )
-                q_codes.append(codes)
-                q_scales.append(scales)
-
-            if h == 0:
-                part_words()
-                quantize(h)
-            else:
-                quantize(h)
-                part_words()
+        for o in range(PASSES):
+            codes = sb.tile([P, NQ], U32, name=f"q_codes{o}", align_bytes=64)
+            scales = sb.tile([P, NQ], U8, name=f"q_scales{o}", align_bytes=64)
+            nc.vector.quantize_mx(
+                out=codes[:].bitcast(FP8X4), scales=scales[:], in_=q_grouped[o][:].rearrange("p w j -> p (w j)")
+            )
+            q_codes.append(codes)
+            q_scales.append(scales)
+            k_codes[0].append(part_words(0, o))
+        for o in range(PASSES):
+            k_codes[1].append(part_words(1, o))
 
         cells = HALF // SEG
         for h in range(HALVES):
             acc = ps.tile([P, HALF], F32, name=f"acc{h}")
             for o in range(PASSES):
+                first = o * N + h * HALF
                 nc.tensor.matmul_mx(
                     out=acc[:],
                     lhsT=q_codes[o][:].bitcast(FP8X4),
                     lhsT_scale=q_scales[o][:],
                     rhs=k_codes[h][o][:].bitcast(FP4X4),
-                    rhs_scale=k_planes[h][:].bitcast(U8)[:, o * HALF : (o + 1) * HALF],
+                    rhs_scale=k_planes[:].bitcast(U8)[:, first : first + HALF],
                     start=(o == 0),
                     stop=(o == PASSES - 1),
                 )

@@ -46,6 +46,9 @@ def tile_attend_celldist_kernel(tc, qT, k_words, k_scales, kn, qn, offs, out):
         def at(offset, shape, dtype, name):
             return shared.tile(shape, dtype, name=name, offset=offset, align_bytes=64)
 
+        def bank(b, shape, name):
+            return ps.tile(shape, F32, name=name, offset=2048 * b)
+
         offsets = sb.tile([P, N // 16], U16, name="offsets")
         nc.sync.dma_start(offsets[:], offs)
         kn_win = sb.tile([P, T], F32, name="kn_win")
@@ -74,12 +77,12 @@ def tile_attend_celldist_kernel(tc, qT, k_words, k_scales, kn, qn, offs, out):
         def spread_norms(h):
             picked = at(KN_PICKED_AT[h], [P, HALF], F32, f"kn_picked{h}")
             nc.vector.tensor_copy(picked[:], kn_win[:].indirect(half_offsets(h)))
-            turned = ps.tile([P, BLOCKS, P], F32, name=f"kn_turned{h}")
+            turned = bank(h, [P, BLOCKS, P], f"kn_turned{h}")
             for m in range(BLOCKS):
                 nc.tensor.transpose(turned[:, m, :], picked[:, m * P : (m + 1) * P], ident[:])
             col = sb.tile([P, BLOCKS], F32, name=f"kn_col{h}")
             nc.scalar.copy(col[:], turned[:, :, KN_ROW])
-            spread = ps.tile([P, BLOCKS, P], F32, name=f"kn_spread{h}")
+            spread = bank(HALVES + h, [P, BLOCKS, P], f"kn_spread{h}")
             for m in range(BLOCKS):
                 nc.tensor.transpose(spread[:, m, :], col[:, m : m + 1].to_broadcast([P, P]), ident[:])
             return spread
@@ -96,7 +99,9 @@ def tile_attend_celldist_kernel(tc, qT, k_words, k_scales, kn, qn, offs, out):
         q_grouped = []
         for o in range(PASSES):
             grouped = sb.tile([P, NQ, 4], BF16, name=f"q_grouped{o}", align_bytes=64)
-            nc.scalar.copy(grouped[:], q_raw[o][:].rearrange("p j w -> p w j"))
+            nc.scalar.copy(
+                grouped[:].rearrange("p (c i) j -> p c j i", i=4), q_raw[o][:].rearrange("p j (c i) -> p c j i", i=4)
+            )
             q_grouped.append(grouped)
         kq = []
         for h in range(HALVES):
@@ -133,23 +138,25 @@ def tile_attend_celldist_kernel(tc, qT, k_words, k_scales, kn, qn, offs, out):
 
         cells = HALF // SEG
         for h in range(HALVES):
-            acc = ps.tile([P, HALF], F32, name=f"acc{h}")
+            accs = [bank((BLOCKS * (h + 1) + m) % 8, [P, P], f"acc{h}_{m}") for m in range(BLOCKS)]
             for o in range(PASSES):
-                first = o * N + h * HALF
-                nc.tensor.matmul_mx(
-                    out=acc[:],
-                    lhsT=q_codes[o][:].bitcast(FP8X4),
-                    lhsT_scale=q_scales[o][:],
-                    rhs=k_codes[h][o][:].bitcast(FP4X4),
-                    rhs_scale=k_planes[:].bitcast(U8)[:, first : first + HALF],
-                    start=(o == 0),
-                    stop=(o == PASSES - 1),
-                )
+                for m in range(BLOCKS):
+                    first = o * N + h * HALF + m * P
+                    nc.tensor.matmul_mx(
+                        out=accs[m][:],
+                        lhsT=q_codes[o][:].bitcast(FP8X4),
+                        lhsT_scale=q_scales[o][:],
+                        rhs=k_codes[h][o][:, m * P : (m + 1) * P].bitcast(FP4X4),
+                        rhs_scale=k_planes[:].bitcast(U8)[:, first : first + P],
+                        start=(o == 0),
+                        stop=(o == PASSES - 1),
+                    )
             dist = sb.tile([P, HALF], F32, name=f"dist{h}")
             least = sb.tile([P, cells], F32, name=f"least{h}")
             pieces = [slice(c, c + PIECE) for c in range(0, HALF, PIECE)]
-            for cols in pieces:
-                nc.vector.scalar_tensor_tensor(dist[:, cols], acc[:, cols], -2.0, kq[h][:, cols], ALU.mult, ALU.add)
+            for m in range(BLOCKS):
+                cols = slice(m * P, (m + 1) * P)
+                nc.vector.scalar_tensor_tensor(dist[:, cols], accs[m][:], -2.0, kq[h][:, cols], ALU.mult, ALU.add)
             for cols in pieces:
                 nc.vector.tensor_reduce(
                     least[:, cols.start // SEG : cols.stop // SEG],

@@ -62,8 +62,6 @@ def tile_attend_celldist_kernel(tc, qT, k_words, k_scales, kn, qn, offs, out):
             raw = at(RAW_AT[o], [P, 4, NQ], F32, f"q_raw{o}")
             nc.sync.dma_start(raw[:], qT[0, 512 * o : 512 * (o + 1), :].rearrange("(p j) w -> p j w", j=4))
             q_raw.append(raw)
-        qn_col = sb.tile([P, 1], F32, name="qn_col")
-        nc.sync.dma_start(qn_col[:], qn[0])
 
         nc.vector.memset(scale_win[0:SC_FIRST, :], 0)
         nc.vector.memset(kn_win[0:KN_ROW, :], 0.0)
@@ -93,7 +91,9 @@ def tile_attend_celldist_kernel(tc, qT, k_words, k_scales, kn, qn, offs, out):
         k_planes = at(SCALE_AT, [P, PASSES * N // 4], I32, "k_planes")
         for quad in range(4):
             first = SC_FIRST + 8 * quad
-            nc.scalar.dma_start(k_planes[32 * quad : 32 * quad + 4, :], scale_picked[first : first + 8, :].bitcast(I32))
+            nc.sync.dma_start(k_planes[32 * quad : 32 * quad + 4, :], scale_picked[first : first + 8, :].bitcast(I32))
+        qn_col = at(SCALE_AT + 2048, [P, 1], F32, "qn_col")
+        nc.sync.dma_start(qn_col[:], qn[0])
         spreads.append(spread_norms(1))
 
         q_grouped = []

@@ -33,6 +33,7 @@ SCALE_AT = 0
 RAW_AT = [4096, 8192]
 PART_AT = [[RAW_AT[0], RAW_AT[1] - 512], [RAW_AT[1] + 512, RAW_AT[1] + 1536]]
 KN_PICKED_AT = [14336, 20480]
+KN_COL_AT = [24576, 28672]
 WORDS_PICKED_AT = [KN_PICKED_AT[0] - 1024, KN_PICKED_AT[0] + 1024]
 
 
@@ -78,8 +79,8 @@ def tile_attend_celldist_kernel(tc, qT, k_words, k_scales, kn, qn, offs, out):
             turned = bank(h, [P, BLOCKS, P], f"kn_turned{h}")
             for m in range(BLOCKS):
                 nc.tensor.transpose(turned[:, m, :], picked[:, m * P : (m + 1) * P], ident[:])
-            col = sb.tile([P, BLOCKS], F32, name=f"kn_col{h}")
-            nc.scalar.copy(col[:], turned[:, :, KN_ROW])
+            col = at(KN_COL_AT[h], [P, 32], F32, f"kn_col{h}")
+            nc.scalar.copy(col[:, 0:BLOCKS], turned[:, :, KN_ROW])
             spread = bank(HALVES + h, [P, BLOCKS, P], f"kn_spread{h}")
             for m in range(BLOCKS):
                 nc.tensor.transpose(spread[:, m, :], col[:, m : m + 1].to_broadcast([P, P]), ident[:])
@@ -98,7 +99,7 @@ def tile_attend_celldist_kernel(tc, qT, k_words, k_scales, kn, qn, offs, out):
 
         q_grouped = []
         for o in range(PASSES):
-            grouped = sb.tile([P, NQ, 4], BF16, name=f"q_grouped{o}", align_bytes=64)
+            grouped = at(KN_COL_AT[0] + 64 + 1024 * (o - 1), [P, NQ, 4], BF16, f"q_grouped{o}")
             nc.scalar.copy(
                 grouped[:].rearrange("p (c i) j -> p c j i", i=4), q_raw[o][:].rearrange("p j (c i) -> p c j i", i=4)
             )
@@ -125,7 +126,7 @@ def tile_attend_celldist_kernel(tc, qT, k_words, k_scales, kn, qn, offs, out):
         q_codes, q_scales = [], []
         k_codes = [[], []]
         for o in range(PASSES):
-            codes = sb.tile([P, NQ], U32, name=f"q_codes{o}", align_bytes=64)
+            codes = at(KN_COL_AT[1] + 512 * o, [P, NQ], U32, f"q_codes{o}")
             scales = sb.tile([P, NQ], U8, name=f"q_scales{o}", align_bytes=64)
             nc.vector.quantize_mx(
                 out=codes[:].bitcast(FP8X4), scales=scales[:], in_=q_grouped[o][:].rearrange("p w j -> p (w j)")

@@ -28,7 +28,7 @@ SC_ROWS = 32
 FLOPS = 2 * NQ * N * D
 BYTES = 4 * D * NQ + 4 * P * T + 2 * 16 * T + 4 * T + 4 * NQ + 2 * P * (N // 16) + 4 * NQ * (N // SEG)
 
-SC_FIRST = P - SC_ROWS
+SC_STEP = P // SC_ROWS
 SCALE_AT = 0
 RAW_AT = [4096, 8192]
 PART_AT = [[RAW_AT[0], RAW_AT[1] - 512], [RAW_AT[1] + 512, RAW_AT[1] + 1536]]
@@ -55,7 +55,8 @@ def tile_attend_celldist_kernel(tc, qT, k_words, k_scales, kn, qn, offs, out):
         kn_win = sb.tile([P, T], F32, name="kn_win")
         nc.scalar.dma_start(kn_win[KN_ROW:P, :], kn[0:1, :])
         scale_win = at(SCALE_AT, [P, T // 4], I32, "scale_win")
-        nc.scalar.dma_start(scale_win[SC_FIRST:P, :], k_scales.bitcast(I32).rearrange("o f t -> f o t"))
+        nc.vector.memset(scale_win[:], 0)
+        nc.scalar.dma_start(scale_win[0:P:SC_STEP, :], k_scales.bitcast(I32).rearrange("o f t -> f o t"))
         word_win = sb.tile([P, T], I32, name="word_win")
         nc.sync.dma_start(word_win[:], k_words[0].rearrange("p t b -> p (t b)").bitcast(I32))
         q_raw = []
@@ -64,7 +65,6 @@ def tile_attend_celldist_kernel(tc, qT, k_words, k_scales, kn, qn, offs, out):
             nc.sync.dma_start(raw[:], qT[0, 512 * o : 512 * (o + 1), :].rearrange("(p j) w -> p j w", j=4))
             q_raw.append(raw)
 
-        nc.vector.memset(scale_win[0:SC_FIRST, :], 0)
         nc.vector.memset(kn_win[0:KN_ROW, :], 0.0)
         ident = sb.tile([P, P], F32, name="ident")
         nc.vector.memset(ident[:], 0.0)
@@ -91,8 +91,8 @@ def tile_attend_celldist_kernel(tc, qT, k_words, k_scales, kn, qn, offs, out):
         nc.vector.tensor_copy(scale_picked[:], scale_win[:].bitcast(U8).indirect(offsets[:]))
         k_planes = at(SCALE_AT, [P, PASSES * N // 4], I32, "k_planes")
         for quad in range(4):
-            first = SC_FIRST + 8 * quad
-            nc.sync.dma_start(k_planes[32 * quad : 32 * quad + 4, :], scale_picked[first : first + 8, :].bitcast(I32))
+            rows = scale_picked[32 * quad : 32 * quad + 32 : SC_STEP, :]
+            nc.sync.dma_start(k_planes[32 * quad : 32 * quad + 4, :], rows.bitcast(I32))
         qn_col = at(SCALE_AT + 2048, [P, 1], F32, "qn_col")
         nc.sync.dma_start(qn_col[:], qn[0])
         spreads.append(spread_norms(1))

@@ -22,6 +22,7 @@ HALF = 512
 HALVES = N // HALF
 BLOCKS = HALF // P
 PIECE = 256
+WORDS_FIRST = 1024
 KN_ROW = P - 1
 SC_ROWS = 32
 
@@ -53,12 +54,14 @@ def tile_attend_celldist_kernel(tc, qT, k_words, k_scales, kn, qn, offs, out):
         offsets = sb.tile([P, N // 16], U16, name="offsets")
         nc.sync.dma_start(offsets[:], offs)
         kn_win = sb.tile([P, T], F32, name="kn_win")
-        nc.scalar.dma_start(kn_win[KN_ROW:P, :], kn[0:1, :])
+        nc.sync.dma_start(kn_win[KN_ROW:P, :], kn[0:1, :])
         scale_win = at(SCALE_AT, [P, T // 4], I32, "scale_win")
-        nc.vector.memset(scale_win[:], 0)
-        nc.scalar.dma_start(scale_win[0:P:SC_STEP, :], k_scales.bitcast(I32).rearrange("o f t -> f o t"))
         word_win = sb.tile([P, T], I32, name="word_win")
-        nc.sync.dma_start(word_win[:], k_words[0].rearrange("p t b -> p (t b)").bitcast(I32))
+        words = k_words[0].rearrange("p t b -> p (t b)").bitcast(I32)
+        nc.sync.dma_start(word_win[:, 0:WORDS_FIRST], words[:, 0:WORDS_FIRST])
+        nc.vector.memset(scale_win[:], 0)
+        nc.sync.dma_start(scale_win[0:P:SC_STEP, :], k_scales.bitcast(I32).rearrange("o f t -> f o t"))
+        nc.sync.dma_start(word_win[:, WORDS_FIRST:T], words[:, WORDS_FIRST:T])
         q_raw = []
         for o in range(PASSES):
             raw = at(RAW_AT[o], [P, 4, NQ], F32, f"q_raw{o}")
@@ -86,7 +89,7 @@ def tile_attend_celldist_kernel(tc, qT, k_words, k_scales, kn, qn, offs, out):
                 nc.tensor.transpose(spread[:, m, :], col[:, m : m + 1].to_broadcast([P, P]), ident[:])
             return spread
 
-        spreads = [spread_norms(0)]
+        spreads = [spread_norms(h) for h in range(HALVES)]
         scale_picked = sb.tile([P, N], U8, name="scale_picked")
         nc.vector.tensor_copy(scale_picked[:], scale_win[:].bitcast(U8).indirect(offsets[:]))
         k_planes = at(SCALE_AT, [P, PASSES * N // 4], I32, "k_planes")
@@ -95,7 +98,6 @@ def tile_attend_celldist_kernel(tc, qT, k_words, k_scales, kn, qn, offs, out):
             nc.sync.dma_start(k_planes[32 * quad : 32 * quad + 4, :], rows.bitcast(I32))
         qn_col = at(SCALE_AT + 2048, [P, 1], F32, "qn_col")
         nc.sync.dma_start(qn_col[:], qn[0])
-        spreads.append(spread_norms(1))
 
         q_grouped = []
         for o in range(PASSES):

@@ -29,7 +29,7 @@ SC_ROWS = 32
 FLOPS = 2 * NQ * N * D
 BYTES = 4 * D * NQ + 4 * P * T + 2 * 16 * T + 4 * T + 4 * NQ + 2 * P * (N // 16) + 4 * NQ * (N // SEG)
 
-SC_STEP = P // SC_ROWS
+SC_FIRST, SC_STEP = 32, 2
 SCALE_AT = 0
 RAW_AT = [4096, 8192]
 PART_AT = [[RAW_AT[0], RAW_AT[1] - 512], [RAW_AT[1] + 512, RAW_AT[1] + 1536]]
@@ -60,7 +60,7 @@ def tile_attend_celldist_kernel(tc, qT, k_words, k_scales, kn, qn, offs, out):
         words = k_words[0].rearrange("p t b -> p (t b)").bitcast(I32)
         nc.sync.dma_start(word_win[:, 0:WORDS_FIRST], words[:, 0:WORDS_FIRST])
         nc.vector.memset(scale_win[:], 0)
-        nc.sync.dma_start(scale_win[0:P:SC_STEP, :], k_scales.bitcast(I32).rearrange("o f t -> f o t"))
+        nc.sync.dma_start(scale_win[SC_FIRST : SC_FIRST + SC_STEP * SC_ROWS : SC_STEP, :], k_scales.bitcast(I32).rearrange("o f t -> f o t"))
         nc.sync.dma_start(word_win[:, WORDS_FIRST:T], words[:, WORDS_FIRST:T])
         q_raw = []
         for o in range(PASSES):
@@ -94,7 +94,8 @@ def tile_attend_celldist_kernel(tc, qT, k_words, k_scales, kn, qn, offs, out):
         nc.vector.tensor_copy(scale_picked[:], scale_win[:].bitcast(U8).indirect(offsets[:]))
         k_planes = at(SCALE_AT, [P, PASSES * N // 4], I32, "k_planes")
         for quad in range(4):
-            rows = scale_picked[32 * quad : 32 * quad + 32 : SC_STEP, :]
+            first = SC_FIRST + 8 * SC_STEP * quad
+            rows = scale_picked[first : first + 8 * SC_STEP : SC_STEP, :]
             nc.sync.dma_start(k_planes[32 * quad : 32 * quad + 4, :], rows.bitcast(I32))
         qn_col = at(SCALE_AT + 2048, [P, 1], F32, "qn_col")
         nc.sync.dma_start(qn_col[:], qn[0])

@@ -32,7 +32,8 @@ BYTES = 4 * D * NQ + 4 * P * T + 2 * 16 * T + 4 * T + 4 * NQ + 2 * P * (N // 16)
 SC_FIRST, SC_STEP = 32, 2
 SCALE_AT = 0
 RAW_AT = [4096, 8192]
-PART_AT = [[RAW_AT[0], RAW_AT[1] - 512], [RAW_AT[1] + 512, RAW_AT[1] + 1536]]
+PART_AT = [[RAW_AT[0], RAW_AT[1] - 960], [RAW_AT[1] + 64, RAW_AT[1] + 1088]]
+KQ_AT = [26624, RAW_AT[1] + 2112]
 KN_PICKED_AT = [14336, 20480]
 KN_COL_AT = [24576, 28672]
 WORDS_PICKED_AT = [KN_PICKED_AT[0] - 1024, KN_PICKED_AT[0] + 1024]
@@ -61,17 +62,24 @@ def tile_attend_celldist_kernel(tc, qT, k_words, k_scales, kn, qn, offs, out):
         nc.sync.dma_start(word_win[:, 0:WORDS_FIRST], words[:, 0:WORDS_FIRST])
         nc.vector.memset(scale_win[:], 0)
         nc.sync.dma_start(scale_win[SC_FIRST : SC_FIRST + SC_STEP * SC_ROWS : SC_STEP, :], k_scales.bitcast(I32).rearrange("o f t -> f o t"))
+        qn_rows = sb.tile([P, P], F32, name="qn_rows")
+        nc.sync.dma_start(qn_rows[KN_ROW:P, :], qn[0].rearrange("q one -> one q"))
         nc.sync.dma_start(word_win[:, WORDS_FIRST:T], words[:, WORDS_FIRST:T])
         q_raw = []
         for o in range(PASSES):
-            raw = at(RAW_AT[o], [P, 4, NQ], F32, f"q_raw{o}")
-            nc.sync.dma_start(raw[:], qT[0, 512 * o : 512 * (o + 1), :].rearrange("(p j) w -> p j w", j=4))
+            raw = at(RAW_AT[o], [P, 5, NQ], F32, f"q_raw{o}")[:, 0:4, :]
+            nc.sync.dma_start(raw, qT[0, 512 * o : 512 * (o + 1), :].rearrange("(p j) w -> p j w", j=4))
             q_raw.append(raw)
 
         nc.vector.memset(kn_win[0:KN_ROW, :], 0.0)
         ident = sb.tile([P, P], F32, name="ident")
         nc.vector.memset(ident[:], 0.0)
         make_identity(nc, ident[:], nomemset=True)
+        nc.vector.memset(qn_rows[0:KN_ROW, :], 0.0)
+        qn_turned = bank(4, [P, P], "qn_turned")
+        nc.tensor.transpose(qn_turned[:], qn_rows[:], ident[:])
+        qn_col = sb.tile([P, 1], F32, name="qn_col")
+        nc.scalar.copy(qn_col[:], qn_turned[:, KN_ROW:P])
 
         def half_offsets(h):
             return offsets[:, h * (HALF // 16) : (h + 1) * (HALF // 16)]
@@ -93,23 +101,21 @@ def tile_attend_celldist_kernel(tc, qT, k_words, k_scales, kn, qn, offs, out):
         scale_picked = sb.tile([P, N], U8, name="scale_picked")
         nc.vector.tensor_copy(scale_picked[:], scale_win[:].bitcast(U8).indirect(offsets[:]))
         k_planes = at(SCALE_AT, [P, PASSES * N // 4], I32, "k_planes")
-        for quad in range(4):
+        for quad in (0, 2, 1, 3):
             first = SC_FIRST + 8 * SC_STEP * quad
             rows = scale_picked[first : first + 8 * SC_STEP : SC_STEP, :]
             nc.sync.dma_start(k_planes[32 * quad : 32 * quad + 4, :], rows.bitcast(I32))
-        qn_col = at(SCALE_AT + 2048, [P, 1], F32, "qn_col")
-        nc.sync.dma_start(qn_col[:], qn[0])
 
         q_grouped = []
         for o in range(PASSES):
             grouped = at(KN_COL_AT[0] + 64 + 1024 * (o - 1), [P, NQ, 4], BF16, f"q_grouped{o}")
             nc.scalar.copy(
-                grouped[:].rearrange("p (c i) j -> p c j i", i=4), q_raw[o][:].rearrange("p j (c i) -> p c j i", i=4)
+                grouped[:].rearrange("p (c i) j -> p c j i", i=4), q_raw[o].rearrange("p j (c i) -> p c j i", i=4)
             )
             q_grouped.append(grouped)
         kq = []
         for h in range(HALVES):
-            both = sb.tile([P, HALF], F32, name=f"kq{h}")
+            both = at(KQ_AT[h], [P, HALF], F32, f"kq{h}")
             nc.scalar.activation(
                 both[:], spreads[h][:].rearrange("p m s -> p (m s)"), ACT.Identity, bias=qn_col[:], scale=1.0
             )

@@ -29,10 +29,10 @@ SC_ROWS = 32
 FLOPS = 2 * NQ * N * D
 BYTES = 4 * D * NQ + 4 * P * T + 2 * 16 * T + 4 * T + 4 * NQ + 2 * P * (N // 16) + 4 * NQ * (N // SEG)
 
-SC_FIRST, SC_STEP = 32, 2
+SC_FIRST, SC_STEP = 28, 2
 SCALE_AT = 0
 RAW_AT = [4096, 8192]
-PART_AT = [[RAW_AT[0], RAW_AT[1] - 960], [RAW_AT[1] + 64, RAW_AT[1] + 1088]]
+PART_AT = [[RAW_AT[0], RAW_AT[0] + 1024], [RAW_AT[1] + 64, RAW_AT[1] + 1088]]
 KQ_AT = [26624, RAW_AT[1] + 2112]
 KN_PICKED_AT = [14336, 20480]
 KN_COL_AT = [24576, 28672]
@@ -132,19 +132,18 @@ def tile_attend_celldist_kernel(tc, qT, k_words, k_scales, kn, qn, offs, out):
             nc.vector.tensor_copy(part[:], pairs[h][:, o, :])
             return part
 
-        q_codes, q_scales = [], []
-        k_codes = [[], []]
-        for o in range(PASSES):
+        def quantise(o):
             codes = at(KN_COL_AT[1] + 512 * o, [P, NQ], U32, f"q_codes{o}")
             scales = sb.tile([P, NQ], U8, name=f"q_scales{o}", align_bytes=64)
             nc.vector.quantize_mx(
                 out=codes[:].bitcast(FP8X4), scales=scales[:], in_=q_grouped[o][:].rearrange("p w j -> p (w j)")
             )
-            q_codes.append(codes)
-            q_scales.append(scales)
-            k_codes[0].append(part_words(0, o))
-        for o in range(PASSES):
-            k_codes[1].append(part_words(1, o))
+            return codes, scales
+
+        q_mx = [quantise(0)]
+        k_codes = [[part_words(0, o) for o in range(PASSES)]]
+        q_mx.append(quantise(1))
+        k_codes.append([part_words(1, o) for o in range(PASSES)])
 
         cells = HALF // SEG
         for h in range(HALVES):
@@ -154,8 +153,8 @@ def tile_attend_celldist_kernel(tc, qT, k_words, k_scales, kn, qn, offs, out):
                     first = o * N + h * HALF + m * P
                     nc.tensor.matmul_mx(
                         out=accs[m][:],
-                        lhsT=q_codes[o][:].bitcast(FP8X4),
-                        lhsT_scale=q_scales[o][:],
+                        lhsT=q_mx[o][0][:].bitcast(FP8X4),
+                        lhsT_scale=q_mx[o][1][:],
                         rhs=k_codes[h][o][:, m * P : (m + 1) * P].bitcast(FP4X4),
                         rhs_scale=k_planes[:].bitcast(U8)[:, first : first + P],
                         start=(o == 0),

@@ -54,6 +54,11 @@ def tile_attend_celldist_kernel(tc, qT, k_words, k_scales, kn, qn, offs, out):
 
         offsets = sb.tile([P, N // 16], U16, name="offsets")
         nc.sync.dma_start(offsets[:], offs)
+        ident = sb.tile([P, P], F32, name="ident")
+        nc.vector.memset(ident[:], 0.0)
+        qn_rows = sb.tile([P, P], F32, name="qn_rows")
+        nc.scalar.copy(qn_rows[0:KN_ROW, :], ident[0:KN_ROW, :])
+        make_identity(nc, ident[:], nomemset=True)
         kn_win = sb.tile([P, T], F32, name="kn_win")
         nc.sync.dma_start(kn_win[KN_ROW:P, :], kn[0:1, :])
         scale_win = at(SCALE_AT, [P, T // 4], I32, "scale_win")
@@ -62,7 +67,6 @@ def tile_attend_celldist_kernel(tc, qT, k_words, k_scales, kn, qn, offs, out):
         nc.sync.dma_start(word_win[:, 0:WORDS_FIRST], words[:, 0:WORDS_FIRST])
         nc.vector.memset(scale_win[:], 0)
         nc.sync.dma_start(scale_win[SC_FIRST : SC_FIRST + SC_STEP * SC_ROWS : SC_STEP, :], k_scales.bitcast(I32).rearrange("o f t -> f o t"))
-        qn_rows = sb.tile([P, P], F32, name="qn_rows")
         nc.sync.dma_start(qn_rows[KN_ROW:P, :], qn[0].rearrange("q one -> one q"))
         nc.sync.dma_start(word_win[:, WORDS_FIRST:T], words[:, WORDS_FIRST:T])
         q_raw = []
@@ -72,10 +76,6 @@ def tile_attend_celldist_kernel(tc, qT, k_words, k_scales, kn, qn, offs, out):
             q_raw.append(raw)
 
         nc.vector.memset(kn_win[0:KN_ROW, :], 0.0)
-        ident = sb.tile([P, P], F32, name="ident")
-        nc.vector.memset(ident[:], 0.0)
-        make_identity(nc, ident[:], nomemset=True)
-        nc.vector.memset(qn_rows[0:KN_ROW, :], 0.0)
         qn_turned = bank(4, [P, P], "qn_turned")
         nc.tensor.transpose(qn_turned[:], qn_rows[:], ident[:])
         qn_col = sb.tile([P, 1], F32, name="qn_col")
@@ -86,7 +86,10 @@ def tile_attend_celldist_kernel(tc, qT, k_words, k_scales, kn, qn, offs, out):
 
         def spread_norms(h):
             picked = at(KN_PICKED_AT[h], [P, HALF], F32, f"kn_picked{h}")
-            nc.vector.tensor_copy(picked[:], kn_win[:].indirect(half_offsets(h)))
+            if h == 0:
+                nc.vector.tensor_copy(picked[:], kn_win[:].indirect(half_offsets(h)))
+            else:
+                nc.scalar.activation(picked[:], kn_win[:].indirect(half_offsets(h)), ACT.Copy)
             turned = bank(h, [P, BLOCKS, P], f"kn_turned{h}")
             for m in range(BLOCKS):
                 nc.tensor.transpose(turned[:, m, :], picked[:, m * P : (m + 1) * P], ident[:])

@@ -32,11 +32,10 @@ BYTES = 4 * D * NQ + 4 * P * T + 2 * 16 * T + 4 * T + 4 * NQ + 2 * P * (N // 16)
 SC_FIRST, SC_STEP = 28, 2
 SCALE_AT = 0
 RAW_AT = [4096, 8192]
-PART_AT = [[RAW_AT[0], RAW_AT[0] + 1024], [RAW_AT[1] + 64, RAW_AT[1] + 1088]]
 KQ_AT = [26624, RAW_AT[1] + 2112]
 KN_PICKED_AT = [14336, 20480]
 KN_COL_AT = [24576, 28672]
-WORDS_PICKED_AT = [KN_PICKED_AT[0] - 1024, KN_PICKED_AT[0] + 1024]
+WORDS_PICKED_AT = KN_PICKED_AT[0] - 1024
 
 
 def tile_attend_celldist_kernel(tc, qT, k_words, k_scales, kn, qn, offs, out):
@@ -53,21 +52,21 @@ def tile_attend_celldist_kernel(tc, qT, k_words, k_scales, kn, qn, offs, out):
             return ps.tile(shape, F32, name=name, offset=2048 * b)
 
         offsets = sb.tile([P, N // 16], U16, name="offsets")
-        nc.sync.dma_start(offsets[:], offs)
-        ident = sb.tile([P, P], F32, name="ident")
-        nc.vector.memset(ident[:], 0.0)
-        qn_rows = sb.tile([P, P], F32, name="qn_rows")
-        nc.scalar.copy(qn_rows[0:KN_ROW, :], ident[0:KN_ROW, :])
-        make_identity(nc, ident[:], nomemset=True)
         kn_win = sb.tile([P, T], F32, name="kn_win")
         nc.sync.dma_start(kn_win[KN_ROW:P, :], kn[0:1, :])
+        qn_rows = sb.tile([P, P], F32, name="qn_rows")
+        nc.scalar.dma_start(qn_rows[KN_ROW:P, :], qn[0].rearrange("q one -> one q"))
+        ident = sb.tile([P, P], F32, name="ident")
+        nc.vector.memset(ident[:], 0.0)
+        nc.scalar.copy(qn_rows[0:KN_ROW, :], ident[0:KN_ROW, :])
+        make_identity(nc, ident[:], nomemset=True)
         scale_win = at(SCALE_AT, [P, T // 4], I32, "scale_win")
         word_win = sb.tile([P, T], I32, name="word_win")
         words = k_words[0].rearrange("p t b -> p (t b)").bitcast(I32)
         nc.sync.dma_start(word_win[:, 0:WORDS_FIRST], words[:, 0:WORDS_FIRST])
+        nc.sync.dma_start(offsets[:], offs)
         nc.vector.memset(scale_win[:], 0)
         nc.sync.dma_start(scale_win[SC_FIRST : SC_FIRST + SC_STEP * SC_ROWS : SC_STEP, :], k_scales.bitcast(I32).rearrange("o f t -> f o t"))
-        nc.sync.dma_start(qn_rows[KN_ROW:P, :], qn[0].rearrange("q one -> one q"))
         nc.sync.dma_start(word_win[:, WORDS_FIRST:T], words[:, WORDS_FIRST:T])
         q_raw = []
         for o in range(PASSES):
@@ -109,6 +108,14 @@ def tile_attend_celldist_kernel(tc, qT, k_words, k_scales, kn, qn, offs, out):
             rows = scale_picked[first : first + 8 * SC_STEP : SC_STEP, :]
             nc.sync.dma_start(k_planes[32 * quad : 32 * quad + 4, :], rows.bitcast(I32))
 
+        def add_norms(h):
+            both = at(KQ_AT[h], [P, HALF], F32, f"kq{h}")
+            nc.scalar.activation(
+                both[:], spreads[h][:].rearrange("p m s -> p (m s)"), ACT.Identity, bias=qn_col[:], scale=1.0
+            )
+            return both
+
+        kq = [add_norms(0)]
         q_grouped = []
         for o in range(PASSES):
             grouped = at(KN_COL_AT[0] + 64 + 1024 * (o - 1), [P, NQ, 4], BF16, f"q_grouped{o}")
@@ -116,24 +123,16 @@ def tile_attend_celldist_kernel(tc, qT, k_words, k_scales, kn, qn, offs, out):
                 grouped[:].rearrange("p (c i) j -> p c j i", i=4), q_raw[o].rearrange("p j (c i) -> p c j i", i=4)
             )
             q_grouped.append(grouped)
-        kq = []
-        for h in range(HALVES):
-            both = at(KQ_AT[h], [P, HALF], F32, f"kq{h}")
-            nc.scalar.activation(
-                both[:], spreads[h][:].rearrange("p m s -> p (m s)"), ACT.Identity, bias=qn_col[:], scale=1.0
-            )
-            kq.append(both)
+        kq.append(add_norms(1))
 
-        pairs = []
-        for h in range(HALVES):
-            words_picked = at(WORDS_PICKED_AT[h], [P, HALF], U32, f"words_picked{h}")
-            nc.vector.tensor_copy(words_picked[:], word_win[:].bitcast(U32).indirect(half_offsets(h)))
-            pairs.append(words_picked[:].bitcast(U16).rearrange("p (n o) -> p o n", o=PASSES))
+        words_picked = at(WORDS_PICKED_AT, [P, N], U32, "words_picked")
+        nc.vector.tensor_copy(words_picked[:], word_win[:].bitcast(U32).indirect(offsets[:]))
+        pairs = words_picked[:].bitcast(U16).rearrange("p (n o) -> p o n", o=PASSES)
 
-        def part_words(h, o):
-            part = at(PART_AT[h][o], [P, HALF], U16, f"k_codes{h}_{o}")
-            nc.vector.tensor_copy(part[:], pairs[h][:, o, :])
-            return part
+        def part_first(o):
+            part = at(RAW_AT[0] + 1024 * o, [P, HALF], U16, f"k_first{o}")
+            nc.vector.tensor_copy(part[:], pairs[:, o, 0:HALF])
+            return part[:]
 
         def quantise(o):
             codes = at(KN_COL_AT[1] + 512 * o, [P, NQ], U32, f"q_codes{o}")
@@ -144,9 +143,11 @@ def tile_attend_celldist_kernel(tc, qT, k_words, k_scales, kn, qn, offs, out):
             return codes, scales
 
         q_mx = [quantise(0)]
-        k_codes = [[part_words(0, o) for o in range(PASSES)]]
+        k_codes = [[part_first(o) for o in range(PASSES)]]
         q_mx.append(quantise(1))
-        k_codes.append([part_words(1, o) for o in range(PASSES)])
+        second = at(RAW_AT[1], [P, PASSES, HALF], U16, "k_second")
+        nc.vector.tensor_copy(second[:], pairs[:, :, HALF:N])
+        k_codes.append([second[:, o, :] for o in range(PASSES)])
 
         cells = HALF // SEG
         for h in range(HALVES):

@@ -22,7 +22,7 @@ HALF = 512
 HALVES = N // HALF
 BLOCKS = HALF // P
 PIECE = 256
-WORDS_FIRST = 1024
+WORDS_FIRST = 512
 KN_ROW = P - 1
 SC_ROWS = 32
 
@@ -89,7 +89,7 @@ def tile_attend_celldist_kernel(tc, qT, k_words, k_scales, kn, qn, offs, out):
                 nc.vector.tensor_copy(picked[:], kn_win[:].indirect(half_offsets(h)))
             else:
                 nc.scalar.activation(picked[:], kn_win[:].indirect(half_offsets(h)), ACT.Copy)
-            turned = bank(h, [P, BLOCKS, P], f"kn_turned{h}")
+            turned = bank(0, [P, BLOCKS, P], f"kn_turned{h}")
             for m in range(BLOCKS):
                 nc.tensor.transpose(turned[:, m, :], picked[:, m * P : (m + 1) * P], ident[:])
             col = at(KN_COL_AT[h], [P, 32], F32, f"kn_col{h}")
@@ -118,7 +118,7 @@ def tile_attend_celldist_kernel(tc, qT, k_words, k_scales, kn, qn, offs, out):
         kq = [add_norms(0)]
         q_grouped = []
         for o in range(PASSES):
-            grouped = at(KN_COL_AT[0] + 64 + 1024 * (o - 1), [P, NQ, 4], BF16, f"q_grouped{o}")
+            grouped = at(KN_PICKED_AT[1] + 1024 * o, [P, NQ, 4], BF16, f"q_grouped{o}")
             nc.scalar.copy(
                 grouped[:].rearrange("p (c i) j -> p c j i", i=4), q_raw[o].rearrange("p j (c i) -> p c j i", i=4)
             )

@@ -131,7 +131,9 @@ def tile_attend_celldist_kernel(tc, qT, k_words, k_scales, kn, qn, offs, out):
 
         def part_first(o):
             part = at(RAW_AT[0] + 1024 * o, [P, HALF], U16, f"k_first{o}")
-            nc.vector.tensor_copy(part[:], pairs[:, o, 0:HALF])
+            cuts = (0, P, HALF) if o == 0 else (0, HALF)
+            for first, last in zip(cuts, cuts[1:]):
+                nc.vector.tensor_copy(part[:, first:last], pairs[:, o, first:last])
             return part[:]
 
         def quantise(o):

@@ -29,7 +29,7 @@ SC_ROWS = 32
 FLOPS = 2 * NQ * N * D
 BYTES = 4 * D * NQ + 4 * P * T + 2 * 16 * T + 4 * T + 4 * NQ + 2 * P * (N // 16) + 4 * NQ * (N // SEG)
 
-SC_FIRST, SC_STEP = 28, 2
+SC_FIRST, SC_STEP = 32, 2
 SCALE_AT = 0
 RAW_AT = [4096, 8192]
 KQ_AT = [26624, RAW_AT[1] + 2112]

from contextlib import ExitStack

import concourse.mybir as mybir
from concourse.masks import make_identity

F32 = mybir.dt.float32
BF16 = mybir.dt.bfloat16
I32 = mybir.dt.int32
U32 = mybir.dt.uint32
U16 = mybir.dt.uint16
U8 = mybir.dt.uint8
FP8X4 = mybir.dt.float8_e4m3fn_x4
FP4X4 = mybir.dt.float4_e2m1fn_x4
ALU = mybir.AluOpType
ACT = mybir.ActivationFunctionType
AXIS = mybir.AxisListType

P = 128
N, T, D, NQ, SEG = 1024, 4096, 1024, 128, 16
PASSES = D // 512
HALF = 512
HALVES = N // HALF
BLOCKS = HALF // P
PIECE = 256
WORDS_FIRST = 512
KN_ROW = P - 1
SC_ROWS = 32

FLOPS = 2 * NQ * N * D
BYTES = 4 * D * NQ + 4 * P * T + 2 * 16 * T + 4 * T + 4 * NQ + 2 * P * (N // 16) + 4 * NQ * (N // SEG)

SC_FIRST, SC_STEP = 32, 2
SCALE_AT = 0
RAW_AT = [4096, 8192]
KQ_AT = [26624, RAW_AT[1] + 2112]
KN_PICKED_AT = [14336, 20480]
KN_COL_AT = [24576, 28672]
WORDS_PICKED_AT = KN_PICKED_AT[0] - 1024


def tile_attend_celldist_kernel(tc, qT, k_words, k_scales, kn, qn, offs, out):
    nc = tc.nc
    with ExitStack() as ctx:
        sb = ctx.enter_context(tc.tile_pool(name="sb", bufs=1))
        shared = ctx.enter_context(tc.tile_pool(name="shared", bufs=1))
        ps = ctx.enter_context(tc.psum_pool(name="ps", bufs=1))

        def at(offset, shape, dtype, name):
            return shared.tile(shape, dtype, name=name, offset=offset, align_bytes=64)

        def bank(b, shape, name):
            return ps.tile(shape, F32, name=name, offset=2048 * b)

        offsets = sb.tile([P, N // 16], U16, name="offsets")
        kn_win = sb.tile([P, T], F32, name="kn_win")
        nc.sync.dma_start(kn_win[KN_ROW:P, :], kn[0:1, :])
        qn_rows = sb.tile([P, P], F32, name="qn_rows")
        nc.scalar.dma_start(qn_rows[KN_ROW:P, :], qn[0].rearrange("q one -> one q"))
        ident = sb.tile([P, P], F32, name="ident")
        nc.vector.memset(ident[:], 0.0)
        nc.scalar.copy(qn_rows[0:KN_ROW, :], ident[0:KN_ROW, :])
        make_identity(nc, ident[:], nomemset=True)
        scale_win = at(SCALE_AT, [P, T // 4], I32, "scale_win")
        word_win = sb.tile([P, T], I32, name="word_win")
        words = k_words[0].rearrange("p t b -> p (t b)").bitcast(I32)
        nc.sync.dma_start(word_win[:, 0:WORDS_FIRST], words[:, 0:WORDS_FIRST])
        nc.sync.dma_start(offsets[:], offs)
        nc.vector.memset(scale_win[:], 0)
        nc.sync.dma_start(scale_win[SC_FIRST : SC_FIRST + SC_STEP * SC_ROWS : SC_STEP, :], k_scales.bitcast(I32).rearrange("o f t -> f o t"))
        nc.sync.dma_start(word_win[:, WORDS_FIRST:T], words[:, WORDS_FIRST:T])
        q_raw = []
        for o in range(PASSES):
            raw = at(RAW_AT[o], [P, 5, NQ], F32, f"q_raw{o}")[:, 0:4, :]
            nc.sync.dma_start(raw, qT[0, 512 * o : 512 * (o + 1), :].rearrange("(p j) w -> p j w", j=4))
            q_raw.append(raw)

        nc.vector.memset(kn_win[0:KN_ROW, :], 0.0)
        qn_turned = bank(4, [P, P], "qn_turned")
        nc.tensor.transpose(qn_turned[:], qn_rows[:], ident[:])
        qn_col = sb.tile([P, 1], F32, name="qn_col")
        nc.scalar.copy(qn_col[:], qn_turned[:, KN_ROW:P])

        def half_offsets(h):
            return offsets[:, h * (HALF // 16) : (h + 1) * (HALF // 16)]

        def spread_norms(h):
            picked = at(KN_PICKED_AT[h], [P, HALF], F32, f"kn_picked{h}")
            if h == 0:
                nc.vector.tensor_copy(picked[:], kn_win[:].indirect(half_offsets(h)))
            else:
                nc.scalar.activation(picked[:], kn_win[:].indirect(half_offsets(h)), ACT.Copy)
            turned = bank(0, [P, BLOCKS, P], f"kn_turned{h}")
            for m in range(BLOCKS):
                nc.tensor.transpose(turned[:, m, :], picked[:, m * P : (m + 1) * P], ident[:])
            col = at(KN_COL_AT[h], [P, 32], F32, f"kn_col{h}")
            nc.scalar.copy(col[:, 0:BLOCKS], turned[:, :, KN_ROW])
            spread = bank(HALVES + h, [P, BLOCKS, P], f"kn_spread{h}")
            for m in range(BLOCKS):
                nc.tensor.transpose(spread[:, m, :], col[:, m : m + 1].to_broadcast([P, P]), ident[:])
            return spread

        spreads = [spread_norms(h) for h in range(HALVES)]
        scale_picked = sb.tile([P, N], U8, name="scale_picked")
        nc.vector.tensor_copy(scale_picked[:], scale_win[:].bitcast(U8).indirect(offsets[:]))
        k_planes = at(SCALE_AT, [P, PASSES * N // 4], I32, "k_planes")
        for quad in (0, 2, 1, 3):
            first = SC_FIRST + 8 * SC_STEP * quad
            rows = scale_picked[first : first + 8 * SC_STEP : SC_STEP, :]
            nc.sync.dma_start(k_planes[32 * quad : 32 * quad + 4, :], rows.bitcast(I32))

        def add_norms(h):
            both = at(KQ_AT[h], [P, HALF], F32, f"kq{h}")
            nc.scalar.activation(
                both[:], spreads[h][:].rearrange("p m s -> p (m s)"), ACT.Identity, bias=qn_col[:], scale=1.0
            )
            return both

        kq = [add_norms(0)]
        q_grouped = []
        for o in range(PASSES):
            grouped = at(KN_PICKED_AT[1] + 1024 * o, [P, NQ, 4], BF16, f"q_grouped{o}")
            nc.scalar.copy(
                grouped[:].rearrange("p (c i) j -> p c j i", i=4), q_raw[o].rearrange("p j (c i) -> p c j i", i=4)
            )
            q_grouped.append(grouped)
        kq.append(add_norms(1))

        words_picked = at(WORDS_PICKED_AT, [P, N], U32, "words_picked")
        nc.vector.tensor_copy(words_picked[:], word_win[:].bitcast(U32).indirect(offsets[:]))
        pairs = words_picked[:].bitcast(U16).rearrange("p (n o) -> p o n", o=PASSES)

        def part_first(o):
            part = at(RAW_AT[0] + 1024 * o, [P, HALF], U16, f"k_first{o}")
            cuts = (0, P, HALF) if o == 0 else (0, HALF)
            for first, last in zip(cuts, cuts[1:]):
                nc.vector.tensor_copy(part[:, first:last], pairs[:, o, first:last])
            return part[:]

        def quantise(o):
            codes = at(KN_COL_AT[1] + 512 * o, [P, NQ], U32, f"q_codes{o}")
            scales = sb.tile([P, NQ], U8, name=f"q_scales{o}", align_bytes=64)
            nc.vector.quantize_mx(
                out=codes[:].bitcast(FP8X4), scales=scales[:], in_=q_grouped[o][:].rearrange("p w j -> p (w j)")
            )
            return codes, scales

        q_mx = [quantise(0)]
        k_codes = [[part_first(o) for o in range(PASSES)]]
        q_mx.append(quantise(1))
        second = at(RAW_AT[1], [P, PASSES, HALF], U16, "k_second")
        nc.vector.tensor_copy(second[:], pairs[:, :, HALF:N])
        k_codes.append([second[:, o, :] for o in range(PASSES)])

        cells = HALF // SEG
        for h in range(HALVES):
            accs = [bank((BLOCKS * (h + 1) + m) % 8, [P, P], f"acc{h}_{m}") for m in range(BLOCKS)]
            for o in range(PASSES):
                for m in range(BLOCKS):
                    first = o * N + h * HALF + m * P
                    nc.tensor.matmul_mx(
                        out=accs[m][:],
                        lhsT=q_mx[o][0][:].bitcast(FP8X4),
                        lhsT_scale=q_mx[o][1][:],
                        rhs=k_codes[h][o][:, m * P : (m + 1) * P].bitcast(FP4X4),
                        rhs_scale=k_planes[:].bitcast(U8)[:, first : first + P],
                        start=(o == 0),
                        stop=(o == PASSES - 1),
                    )
            dist = sb.tile([P, HALF], F32, name=f"dist{h}")
            least = sb.tile([P, cells], F32, name=f"least{h}")
            pieces = [slice(c, c + PIECE) for c in range(0, HALF, PIECE)]
            for m in range(BLOCKS):
                cols = slice(m * P, (m + 1) * P)
                nc.vector.scalar_tensor_tensor(dist[:, cols], accs[m][:], -2.0, kq[h][:, cols], ALU.mult, ALU.add)
            for cols in pieces:
                nc.vector.tensor_reduce(
                    least[:, cols.start // SEG : cols.stop // SEG],
                    dist[:, cols].rearrange("p (c s) -> p c s", s=SEG),
                    AXIS.X,
                    ALU.min,
                )
            nc.sync.dma_start(out[0, :, h * cells : (h + 1) * cells], least[:])
